import numpy as np
import ml_dtypes


def mxq(x, axis, fmt="e4m3"):
    dtype, down = {"e4m3": (ml_dtypes.float8_e4m3fn, 7), "e5m2": (ml_dtypes.float8_e5m2, 14)}[fmt]
    v = np.moveaxis(np.asarray(x, np.float32).astype(ml_dtypes.bfloat16).astype(np.float64), axis, -1)
    blocks = v.reshape(v.shape[:-1] + (-1, 32))
    amax = np.abs(blocks).max(-1, keepdims=True)
    byte = np.maximum(np.where(amax > 0, np.frexp(amax)[1] - 1 + 127, 0) - down, 1)
    scale = np.exp2(byte - 127.0)
    codes = (blocks / scale).astype(np.float32).astype(dtype).astype(np.float64)
    return np.moveaxis((codes * scale).reshape(v.shape), -1, axis)


WIDE = False


def mx_kscale(k):
    if not WIDE:
        return np.ones(k)
    levels = np.array([10, -10, 5, -5, 0])
    if k % 512:
        return np.exp2(np.random.permutation(np.resize(levels, k // 32))).repeat(32)
    a = np.empty((k // 512, 16))
    for p in range(k // 512):
        a[p, :8] = np.random.permutation(np.resize(levels, 8))
        for g in range(8):
            far = levels[np.abs(levels - a[p, g]) >= 10]
            a[p, g + 8] = far[np.random.randint(len(far))]
    return np.exp2(a.ravel()).repeat(32)


def f64(x):
    return np.asarray(x).astype(np.float64)


def striped(idx):
    return np.tile(idx.reshape(-1, 16).T, (8, 1)).astype(np.uint16)


def unstriped(offs):
    return offs[:16].T.reshape(-1).astype(np.int64)


E2M1 = np.array([0.0, 0.5, 1.0, 1.5, 2.0, 3.0, 4.0, 6.0, -0.0, -0.5, -1.0, -1.5, -2.0, -3.0, -4.0, -6.0])


def pack_weight(w, fmt):
    k, n = w.shape
    w = f64(np.asarray(w, np.float32).astype(ml_dtypes.bfloat16)).reshape(k // 32, 32, n)
    amax = np.abs(w).max(1)
    if fmt == "e4m3":
        byte = np.frexp(amax)[1] - 1 + 127 - 7
    else:
        mant, ex = np.frexp(amax / 6.0)
        byte = np.where(mant > 0.5, ex, ex - 1) + 127
    byte = np.clip(np.where(amax > 0, byte, 1), 1, 254)
    scaled = (w * np.exp2(127.0 - byte)[:, None, :]).reshape(k, n).astype(np.float32)
    by_word = np.ascontiguousarray(scaled.reshape(k // 512, 128, 4, n).transpose(0, 1, 3, 2))
    if fmt == "e4m3":
        words = by_word.astype(ml_dtypes.float8_e4m3fn).view(np.uint8)
    else:
        c = by_word.astype(ml_dtypes.float4_e2m1fn).view(np.uint8) & 0xF
        words = (c[..., 0::2] | (c[..., 1::2] << 4)).reshape(k // 512, 128, 2 * n)
    return np.ascontiguousarray(words), np.ascontiguousarray(byte.astype(np.uint8).reshape(k // 512, 16, n))


def unpack_weight(words, scales, fmt):
    g, _, n = scales.shape
    words = np.ascontiguousarray(words).reshape(g, 128, n, -1)
    if fmt == "e4m3":
        vals = words.view(ml_dtypes.float8_e4m3fn).astype(np.float64)
    else:
        nib = np.empty((g, 128, n, 4), np.uint8)
        nib[..., 0::2] = words & 0xF
        nib[..., 1::2] = words >> 4
        vals = E2M1[nib]
    vals = vals * np.repeat(np.exp2(scales.astype(np.float64) - 127.0), 8, axis=1)[..., None]
    return vals.transpose(0, 1, 3, 2).reshape(g * 512, n)


def gelu(v):
    return 0.5 * v * (1.0 + np.tanh(np.sqrt(2.0 / np.pi) * (v + 0.044715 * v**3)))


K, T, S, T2, H, N, P = 1024, 4096, 1024, 2048, 1024, 256, 128

def setup_inputs():
    n = np.random.standard_normal
    s = mx_kscale(K)[:, None]
    u = mx_kscale(H)[:, None]
    tab_words, tab_scales = pack_weight(n((K, T)) * s, "e4m3")
    w2_words, w2_scales = pack_weight(n((H, N)) / np.sqrt(H) / u, "e2m1")
    return {
        "tab_words": tab_words, "tab_scales": tab_scales,
        "offs": striped(np.random.permutation(T)[:S]),
        "w1": (n((K, H)) / np.sqrt(K) / s).astype(np.float32),
        "gain": (np.random.uniform(0.8, 1.6, H) * u[:, 0]).astype(np.float32),
        "wgs": np.exp(0.3 * n((P, S))).astype(np.float32),
        "offs2": striped(np.random.permutation(T2)[:S]),
        "old": (n((H, T2)) * u).astype(np.float32),
        "w2_words": w2_words, "w2_scales": w2_scales,
    }

def reference(tab_words, tab_scales, offs, w1, gain, wgs, offs2, old, w2_words, w2_scales):
    v = unpack_weight(tab_words, tab_scales, "e4m3")[:, unstriped(offs)]
    w1q = mxq(f64(w1), 0, "e4m3")
    a = w1q.T @ v
    h = np.tanh(a) * f64(gain)[:, None]
    page = np.zeros((H, T2))
    page[:, unstriped(offs2)] = np.tile(f64(wgs), (H // P, 1)) * h
    z = np.abs(page - f64(old))
    zq = mxq(z, 0, "e4m3")
    w2 = unpack_weight(w2_words, w2_scales, "e2m1")
    return w2.T @ zq

@@ -1,0 +1,306 @@
+from contextlib import ExitStack
+
+import concourse.mybir as mybir
+from concourse.masks import make_identity
+
+K, T, S, T2, H, N, P = 1024, 4096, 1024, 2048, 1024, 256, 128
+FLOPS = 2 * K * H * S + 2 * H * N * T2
+
+F32 = mybir.dt.float32
+BF16 = mybir.dt.bfloat16
+I32 = mybir.dt.int32
+U32 = mybir.dt.uint32
+U16 = mybir.dt.uint16
+U8 = mybir.dt.uint8
+FP8X4 = mybir.dt.float8_e4m3fn_x4
+FP4X4 = mybir.dt.float4_e2m1fn_x4
+ACT = mybir.ActivationFunctionType
+ALU = mybir.AluOpType
+
+BANK = 512
+HALF = S // 2
+CHUNKS = T2 // BANK
+PAGES = 3
+
+
+def tile_list_replay_slot_priority_kernel(
+    tc, tab_words, tab_scales, offs, w1, gain, wgs, offs2, old, w2_words, w2_scales, out
+):
+    nc = tc.nc
+    with ExitStack() as ctx:
+        keep = ctx.enter_context(tc.tile_pool(name="keep", bufs=1))
+        psum = ctx.enter_context(tc.psum_pool(name="psum", bufs=1))
+
+        def sb(name, shape, dtype, tag=None, bufs=1):
+            return keep.tile(shape, dtype, name=name, tag=tag or name, bufs=bufs, align_bytes=64)
+
+        def bank(b, name):
+            return psum.tile([P, BANK], F32, name=name, tag="bank%d" % b)
+
+        pick = sb("pick", [P, S // 16], U16)
+        place = sb("place", [P, S // 16], U16)
+        nc.sync.dma_start(pick[:], offs)
+        nc.sync.dma_start(place[:], offs2)
+        gain_rows = sb("gain_rows", [P, 4], F32)
+        with nc.allow_non_contiguous_dma(reason="one gain a partition"):
+            nc.sync.dma_start(gain_rows[:], gain[0:512].rearrange("(m p) -> p m", p=P))
+        gain_dealt = sb("gain_dealt", [P, 4], F32)
+        nc.sync.dma_start(gain_dealt[:], gain[512:1024].rearrange("(p i) -> p i", i=4))
+
+        tab_plane = sb("tab_plane", [P, T], U8)
+        nc.vector.memset(tab_plane[:].bitcast(I32), 0)
+        for q in range(4):
+            nc.scalar.dma_start(
+                tab_plane[32 * q : 32 * q + 8, :].bitcast(I32),
+                tab_scales[:, 4 * q : 4 * q + 4, :].bitcast(I32),
+            )
+
+        words = [sb("words%d" % a, [P, T], U32, tag="big%d" % a) for a in range(2)]
+
+        def load_words(a):
+            nc.sync.dma_start(
+                words[a][:].bitcast(I32), tab_words[a].rearrange("p t i -> p (t i)").bitcast(I32)
+            )
+
+        def load_w1(name, a, c0, width, tag=None):
+            raw = sb(name, [P, 4, width], F32, tag=tag)
+            nc.sync.dma_start(
+                raw[:], w1[512 * a : 512 * (a + 1), c0 : c0 + width].rearrange("(p j) c -> p j c", j=4)
+            )
+            return raw
+
+        load_words(0)
+        raw_first = [load_w1("raw_first%d" % a, a, 0, 128) for a in range(2)]
+        load_words(1)
+        wgs_rows = sb("wgs_rows", [P, S], F32)
+        nc.sync.dma_start(wgs_rows[:], wgs)
+        raw_second = [load_w1("raw_second%d" % a, a, 128, 128) for a in range(2)]
+        raw_third = [load_w1("raw_third%d" % a, a, 256, 256) for a in range(2)]
+        raw_dealt = [load_w1("raw_dealt%d" % a, a, 512, 512, tag="mid%d" % a) for a in range(2)]
+
+        pages = [sb("page%d" % i, [P, T2], F32) for i in range(PAGES)]
+        for page in pages:
+            nc.vector.memset(page[:], 0.0)
+        ident = sb("ident", [P, P], F32)
+        make_identity(nc, ident[:])
+        w2_plane = sb("w2_plane", [P, 2, N], U8)
+        nc.vector.memset(w2_plane[:].rearrange("p a c -> p (a c)").bitcast(I32), 0)
+
+        def load_old_rows(m):
+            rows = sb("old_rows%d" % m, [P, T2], F32, tag="old_rows", bufs=3)
+            nc.sync.dma_start(rows[:], old[P * m : P * (m + 1), :])
+            return rows
+
+        old_rows = [load_old_rows(m) for m in range(3)]
+
+        v0 = sb("v0", [P, S], U32)
+        v1 = [sb("v1_%d" % s, [P, HALF], U32) for s in range(2)]
+        v_plane = sb("v_plane", [P, S], U8)
+        nc.vector.tensor_copy(v0[:], words[0][:].indirect(pick[:]))
+        nc.vector.tensor_copy(v_plane[:], tab_plane[:].indirect(pick[:]))
+
+        def quantize_natural(m):
+            raw, c0 = ((raw_first, 0), (raw_second, 0), (raw_third, 0), (raw_third, P))[m]
+            grouped = sb("grouped%d" % m, [P, 2, P * 4], BF16, tag="grouped", bufs=2)
+            for a in range(2):
+                nc.scalar.copy(
+                    grouped[:, a, :].rearrange("p (c i j) -> p c j i", i=4, j=4),
+                    raw[a][:, :, c0 : c0 + P].rearrange("p j (c i) -> p c j i", i=4),
+                )
+            codes = sb("w1_codes%d" % m, [P, 2 * P], U32)
+            plane = sb("w1_plane%d" % m, [P, 2 * P], U8)
+            nc.vector.quantize_mx(
+                out=codes[:].bitcast(FP8X4), scales=plane[:], in_=grouped[:].rearrange("p a c -> p (a c)")
+            )
+            return [(codes[:, P * a : P * (a + 1)], plane[:, P * a : P * (a + 1)]) for a in range(2)]
+
+        def quantize_dealt(a):
+            grouped = sb("grouped_dealt%d" % a, [P, 2048], BF16)
+            dst = grouped[:].rearrange("p (t m j) -> p m j t", t=4, j=4)
+            src = raw_dealt[a][:].rearrange("p j (m t) -> p m j t", t=4)
+            for s in range(2):
+                nc.scalar.copy(dst[:, 64 * s : 64 * (s + 1)], src[:, 64 * s : 64 * (s + 1)])
+            codes = sb("w1_codes_dealt%d" % a, [P, 512], U32)
+            plane = sb("w1_plane_dealt%d" % a, [P, 512], U8)
+            nc.vector.quantize_mx(out=codes[:].bitcast(FP8X4), scales=plane[:], in_=grouped[:])
+            return [(codes[:, P * i : P * (i + 1)], plane[:, P * i : P * (i + 1)]) for i in range(4)]
+
+        stationary = {0: quantize_natural(0)}
+        for s in range(2):
+            nc.vector.tensor_copy(v1[s][:], words[1][:].indirect(pick[:, 32 * s : 32 * (s + 1)]))
+
+        def first_stage_half(m, s, h):
+            acc = bank(s, "acc%d_%d" % (m, s))
+            cols = slice(HALF * s, HALF * (s + 1))
+            for a in range(2):
+                codes, plane = stationary[m][a]
+                moving = v0[:, cols] if a == 0 else v1[s][:]
+                nc.tensor.matmul_mx(
+                    out=acc[:],
+                    lhsT=codes.bitcast(FP8X4),
+                    lhsT_scale=plane,
+                    rhs=moving.bitcast(FP8X4),
+                    rhs_scale=v_plane[4 * a : P, cols],
+                    start=(a == 0),
+                    stop=(a == 1),
+                )
+            nc.scalar.activation(h[:, cols], acc[:], ACT.Tanh, scale=-1.0)
+
+        def gain_of(m):
+            return gain_rows[:, m : m + 1] if m < 4 else gain_dealt[:, m - 4 : m - 3]
+
+        def first_stage(m):
+            h = sb("h%d" % m, [P, S], F32, tag="h", bufs=3)
+            for s in range(2):
+                first_stage_half(m, s, h)
+            nc.scalar.activation(h[:], h[:], ACT.Copy, scale=gain_of(m))
+            return h
+
+        def scatter(m, h, weights):
+            nc.vector.tensor_tensor(pages[m % PAGES][:].indirect(place[:]), h[:], weights, ALU.mult)
+
+        h_first = sb("h0", [P, S], F32, tag="h", bufs=3)
+        for s in range(2):
+            cols = slice(HALF * s, HALF * (s + 1))
+            first_stage_half(0, s, h_first)
+            nc.scalar.activation(h_first[:, cols], h_first[:, cols], ACT.Copy, scale=gain_of(0))
+            nc.vector.tensor_tensor(
+                pages[0][:].indirect(place[:, 32 * s : 32 * (s + 1)]), h_first[:, cols], wgs_rows[:, cols], ALU.mult
+            )
+            if s == 0:
+                stationary[1] = quantize_natural(1)
+
+        turned = [sb("turned%d" % c, [P, 4, 512], BF16) for c in range(CHUNKS)]
+
+        def difference_turned(m):
+            page = pages[m % PAGES]
+            for c in range(CHUNKS):
+                acc = bank(2 + c, "fwd%d_%d" % (m, c))
+                for step, source in enumerate((old_rows[m], page)):
+                    for b in range(4):
+                        t0 = BANK * c + P * b
+                        nc.tensor.matmul(
+                            acc[:, P * b : P * (b + 1)],
+                            lhsT=source[:, t0 : t0 + P],
+                            rhs=ident[:],
+                            is_transpose=True,
+                            start=(step == 0 and b == 0),
+                            stop=(step == 1 and b == 3),
+                        )
+                nc.scalar.activation(
+                    turned[c][:, :, P * m : P * (m + 1)], acc[:].rearrange("p (b r) -> p b r", b=4), ACT.Abs
+                )
+
+        def quantize_z(g, c, z):
+            codes = sb("z_codes%d_%d" % (g, c), [P, BANK], U32)
+            plane = sb("z_plane%d_%d" % (g, c), [P, BANK], U8)
+            nc.vector.quantize_mx(out=codes[:].bitcast(FP8X4), scales=plane[:], in_=z[:])
+            return codes, plane
+
+        def turn_back(c):
+            z = sb("z0_%d" % c, [P, 4 * BANK], BF16, tag="z", bufs=4)
+            for half in range(2):
+                acc = bank(6 + half, "back%d_%d" % (c, half))
+                for b in range(2):
+                    pairs = turned[c][:, 2 * half + b, :].bitcast(F32)
+                    for u in range(2):
+                        col = P * (2 * b + u)
+                        nc.tensor.transpose(acc[:, col : col + P], pairs[:, u:256:2], ident[:])
+                nc.scalar.copy(
+                    z[:, 1024 * half : 1024 * (half + 1)].bitcast(F32).rearrange("p (b t u) -> p b t u", b=2, u=2),
+                    acc[:].rearrange("p (b u t) -> p b t u", b=2, u=2),
+                )
+            return quantize_z(0, c, z)
+
+        stationary[2] = quantize_natural(2)
+        stationary[3] = quantize_natural(3)
+        h1 = first_stage(1)
+        scatter(1, h1, wgs_rows[:])
+        dealt0 = quantize_dealt(0)
+        h2 = first_stage(2)
+        scatter(2, h2, wgs_rows[:])
+        dealt1 = quantize_dealt(1)
+        for i in range(4):
+            stationary[4 + i] = [dealt0[i], dealt1[i]]
+
+        wgs_dealt = sb("wgs_dealt", [P, 4, S], F32, tag="big1")
+        for q in range(4):
+            nc.sync.dma_start(wgs_dealt[32 * q : 32 * (q + 1)], wgs.rearrange("(m i) s -> m i s", i=4))
+        old_rows.append(load_old_rows(3))
+        old_dealt = old[512:1024, :].rearrange("(p u e) t -> u p e t", u=2, e=2)
+        old_low = sb("old_low", [P, 2, T2], F32, tag="big0")
+        nc.sync.dma_start(old_low[:], old_dealt[0])
+        w2_codes = sb("w2_codes", [P, 2, 2 * N], U8)
+        nc.sync.dma_start(w2_codes[:].bitcast(I32), w2_words.rearrange("a p c -> p a c").bitcast(I32))
+        for q in range(4):
+            nc.sync.dma_start(
+                w2_plane[32 * q : 32 * q + 4].bitcast(I32),
+                w2_scales[:, 4 * q : 4 * q + 4, :].rearrange("a r c -> r a c").bitcast(I32),
+            )
+        old_high = []
+        for c in range(CHUNKS):
+            piece = sb("old_high%d" % c, [P, 2, BANK], F32)
+            nc.sync.dma_start(piece[:], old_dealt[1][:, :, BANK * c : BANK * (c + 1)])
+            old_high.append(piece)
+
+        difference_turned(0)
+        h3 = first_stage(3)
+        scatter(3, h3, wgs_rows[:])
+        difference_turned(1)
+        h4 = first_stage(4)
+        scatter(4, h4, wgs_dealt[:, 0, :])
+        nc.vector.tensor_tensor(old_low[:, 0, :], old_low[:, 0, :], pages[4 % PAGES][:], ALU.add)
+        difference_turned(2)
+        h5 = first_stage(5)
+        scatter(5, h5, wgs_dealt[:, 1, :])
+        nc.vector.tensor_tensor(old_low[:, 1, :], old_low[:, 1, :], pages[5 % PAGES][:], ALU.add)
+        h6 = first_stage(6)
+        difference_turned(3)
+        scatter(6, h6, wgs_dealt[:, 2, :])
+        for c in range(CHUNKS):
+            cols = slice(BANK * c, BANK * (c + 1))
+            nc.vector.tensor_tensor(old_high[c][:, 0, :], old_high[c][:, 0, :], pages[6 % PAGES][:, cols], ALU.add)
+        h7 = first_stage(7)
+        z_first = [turn_back(c) for c in range(CHUNKS)]
+        scatter(7, h7, wgs_dealt[:, 3, :])
+
+        def second_pass(acc, g, n, z):
+            codes, plane = z
+            nc.tensor.matmul_mx(
+                out=acc[:],
+                lhsT=w2_codes[:, g, 2 * P * n : 2 * P * (n + 1)].bitcast(FP4X4),
+                lhsT_scale=w2_plane[:, g, P * n : P * (n + 1)],
+                rhs=codes[:].bitcast(FP8X4),
+                rhs_scale=plane[:],
+                start=(g == 0),
+                stop=(g == 1),
+            )
+
+        def absolute_pair(z, u, pair):
+            nc.scalar.activation(
+                z[:].rearrange("p (t u e) -> p u t e", u=2, e=2)[:, u], pair.rearrange("p e t -> p t e"), ACT.Abs
+            )
+
+        sums = {}
+        z_second = []
+        for c in range(CHUNKS):
+            for n in range(2):
+                sums[c, n] = bank((2 + 2 * c + n) % 8, "sum%d_%d" % (c, n))
+                second_pass(sums[c, n], 0, n, z_first[c])
+            z = sb("z1_%d" % c, [P, 4 * BANK], BF16, tag="z", bufs=4)
+            absolute_pair(z, 0, old_low[:, :, BANK * c : BANK * (c + 1)])
+            z_second.append(z)
+
+        staged = [sb("staged%d" % n, [P, CHUNKS, BANK], F32, tag="mid%d" % n) for n in range(2)]
+        for c in range(CHUNKS):
+            cols = slice(BANK * c, BANK * (c + 1))
+            nc.vector.tensor_tensor(old_high[c][:, 1, :], old_high[c][:, 1, :], pages[7 % PAGES][:, cols], ALU.add)
+            absolute_pair(z_second[c], 1, old_high[c][:])
+            z = quantize_z(1, c, z_second[c])
+            for n in range(2):
+                second_pass(sums[c, n], 1, n, z)
+                if n == 1 and c >= 2:
+                    nc.scalar.copy(staged[n][:, c, :], sums[c, n][:])
+                else:
+                    nc.vector.tensor_copy(staged[n][:, c, :], sums[c, n][:])
+                nc.sync.dma_start(out[P * n : P * (n + 1), cols], staged[n][:, c, :])

@@ -21,6 +21,7 @@ BANK = 512
 HALF = S // 2
 CHUNKS = T2 // BANK
 PAGES = 3
+PIECES = [(0, 512), (512, 512), (1024, 512), (1536, 256), (1792, 256)]
 
 
 def tile_list_replay_slot_priority_kernel(
@@ -34,32 +35,28 @@ def tile_list_replay_slot_priority_kernel(
         def sb(name, shape, dtype, tag=None, bufs=1):
             return keep.tile(shape, dtype, name=name, tag=tag or name, bufs=bufs, align_bytes=64)
 
-        def bank(b, name):
-            return psum.tile([P, BANK], F32, name=name, tag="bank%d" % b)
+        def bank(b, name, dtype=F32, width=BANK):
+            return psum.tile([P, width], dtype, name=name, tag="bank%d" % b)
 
+        tab_plane = sb("tab_plane", [P, T], U8)
+        nc.vector.memset(tab_plane[:, 0 : T // 2].bitcast(I32), 0)
+        nc.gpsimd.memset(tab_plane[:, T // 2 : T].bitcast(I32), 0)
         pick = sb("pick", [P, S // 16], U16)
         place = sb("place", [P, S // 16], U16)
         nc.sync.dma_start(pick[:], offs)
         nc.sync.dma_start(place[:], offs2)
-        gain_rows = sb("gain_rows", [P, 4], F32)
-        with nc.allow_non_contiguous_dma(reason="one gain a partition"):
-            nc.sync.dma_start(gain_rows[:], gain[0:512].rearrange("(m p) -> p m", p=P))
+        gain_flat = sb("gain_flat", [P, P], F32)
+        nc.gpsimd.memset(gain_flat[:], 0.0)
         gain_dealt = sb("gain_dealt", [P, 4], F32)
         nc.sync.dma_start(gain_dealt[:], gain[512:1024].rearrange("(p i) -> p i", i=4))
+        nc.sync.dma_start(gain_flat[0:4, :], gain[0:512].rearrange("(m p) -> m p", p=P))
 
-        tab_plane = sb("tab_plane", [P, T], U8)
-        nc.vector.memset(tab_plane[:].bitcast(I32), 0)
-        for q in range(4):
-            nc.scalar.dma_start(
-                tab_plane[32 * q : 32 * q + 8, :].bitcast(I32),
-                tab_scales[:, 4 * q : 4 * q + 4, :].bitcast(I32),
-            )
 
         words = [sb("words%d" % a, [P, T], U32, tag="big%d" % a) for a in range(2)]
 
-        def load_words(a):
+        def load_words(a, cols):
             nc.sync.dma_start(
-                words[a][:].bitcast(I32), tab_words[a].rearrange("p t i -> p (t i)").bitcast(I32)
+                words[a][:, cols].bitcast(I32), tab_words[a].rearrange("p t i -> p (t i)").bitcast(I32)[:, cols]
             )
 
         def load_w1(name, a, c0, width, tag=None):
@@ -69,20 +66,34 @@ def tile_list_replay_slot_priority_kernel(
             )
             return raw
 
-        load_words(0)
+        for piece in range(4):
+            load_words(0, slice(piece * T // 4, (piece + 1) * T // 4))
         raw_first = [load_w1("raw_first%d" % a, a, 0, 128) for a in range(2)]
-        load_words(1)
         wgs_rows = sb("wgs_rows", [P, S], F32)
         nc.sync.dma_start(wgs_rows[:], wgs)
+        for q in range(4):
+            nc.sync.dma_start(
+                tab_plane[32 * q : 32 * q + 8, :].bitcast(I32),
+                tab_scales[:, 4 * q : 4 * q + 4, :].bitcast(I32),
+            )
+        load_words(1, slice(0, T))
         raw_second = [load_w1("raw_second%d" % a, a, 128, 128) for a in range(2)]
-        raw_third = [load_w1("raw_third%d" % a, a, 256, 256) for a in range(2)]
+        raw_third = [load_w1("raw_third%d" % a, a, 256, 256, tag="turned%d" % a) for a in range(2)]
         raw_dealt = [load_w1("raw_dealt%d" % a, a, 512, 512, tag="mid%d" % a) for a in range(2)]
 
         pages = [sb("page%d" % i, [P, T2], F32) for i in range(PAGES)]
-        for page in pages:
+        for page in pages[:2]:
             nc.vector.memset(page[:], 0.0)
         ident = sb("ident", [P, P], F32)
         make_identity(nc, ident[:])
+        ident_bf = sb("ident_bf", [P, P], BF16)
+        make_identity(nc, ident_bf[:])
+        for page in pages[2:]:
+            nc.gpsimd.memset(page[:], 0.0)
+        gain_rows = sb("gain_rows", [P, 4], F32)
+        gain_bank = bank(6, "gain_bank")
+        nc.tensor.transpose(gain_bank[:, 0:P], gain_flat[:], ident[:])
+        nc.scalar.copy(gain_rows[:], gain_bank[:, 0:4])
         w2_plane = sb("w2_plane", [P, 2, N], U8)
         nc.vector.memset(w2_plane[:].rearrange("p a c -> p (a c)").bitcast(I32), 0)
 
@@ -114,23 +125,33 @@ def tile_list_replay_slot_priority_kernel(
             )
             return [(codes[:, P * a : P * (a + 1)], plane[:, P * a : P * (a + 1)]) for a in range(2)]
 
-        def quantize_dealt(a):
-            grouped = sb("grouped_dealt%d" % a, [P, 2048], BF16)
-            dst = grouped[:].rearrange("p (t m j) -> p m j t", t=4, j=4)
-            src = raw_dealt[a][:].rearrange("p j (m t) -> p m j t", t=4)
-            for s in range(2):
-                nc.scalar.copy(dst[:, 64 * s : 64 * (s + 1)], src[:, 64 * s : 64 * (s + 1)])
-            codes = sb("w1_codes_dealt%d" % a, [P, 512], U32)
-            plane = sb("w1_plane_dealt%d" % a, [P, 512], U8)
-            nc.vector.quantize_mx(out=codes[:].bitcast(FP8X4), scales=plane[:], in_=grouped[:])
-            return [(codes[:, P * i : P * (i + 1)], plane[:, P * i : P * (i + 1)]) for i in range(4)]
+        def quantize_dealt(u):
+            grouped = sb("grouped_dealt%d" % u, [P, 2, 1024], BF16)
+            for a in range(2):
+                nc.scalar.copy(
+                    grouped[:, a, :].rearrange("p (e m j) -> p m j e", e=2, j=4),
+                    raw_dealt[a][:].rearrange("p j (m u e) -> p u m j e", u=2, e=2)[:, u],
+                )
+            codes = sb("w1_codes_dealt%d" % u, [P, 512], U32)
+            plane = sb("w1_plane_dealt%d" % u, [P, 512], U8)
+            nc.vector.quantize_mx(
+                out=codes[:].bitcast(FP8X4), scales=plane[:], in_=grouped[:].rearrange("p a c -> p (a c)")
+            )
+            for e in range(2):
+                spans = [slice(P * (2 * a + e), P * (2 * a + e + 1)) for a in range(2)]
+                stationary[4 + 2 * u + e] = [(codes[:, span], plane[:, span]) for span in spans]
 
         stationary = {0: quantize_natural(0)}
+        weights = []
+        for m in range(4):
+            scaled = sb("weights%d" % m, [P, S], F32, tag="z", bufs=4)
+            nc.vector.tensor_scalar_mul(scaled[:], wgs_rows[:], gain_rows[:, m : m + 1])
+            weights.append(scaled)
         for s in range(2):
             nc.vector.tensor_copy(v1[s][:], words[1][:].indirect(pick[:, 32 * s : 32 * (s + 1)]))
 
         def first_stage_half(m, s, h):
-            acc = bank(s, "acc%d_%d" % (m, s))
+            acc = bank(2 * (m % 3) + s, "acc%d_%d" % (m, s))
             cols = slice(HALF * s, HALF * (s + 1))
             for a in range(2):
                 codes, plane = stationary[m][a]
@@ -146,66 +167,96 @@ def tile_list_replay_slot_priority_kernel(
                 )
             nc.scalar.activation(h[:, cols], acc[:], ACT.Tanh, scale=-1.0)
 
-        def gain_of(m):
-            return gain_rows[:, m : m + 1] if m < 4 else gain_dealt[:, m - 4 : m - 3]
-
         def first_stage(m):
             h = sb("h%d" % m, [P, S], F32, tag="h", bufs=3)
             for s in range(2):
                 first_stage_half(m, s, h)
-            nc.scalar.activation(h[:], h[:], ACT.Copy, scale=gain_of(m))
+            if m >= 4:
+                nc.scalar.activation(h[:], h[:], ACT.Copy, scale=gain_dealt[:, m - 4 : m - 3])
             return h
 
-        def scatter(m, h, weights):
-            nc.vector.tensor_tensor(pages[m % PAGES][:].indirect(place[:]), h[:], weights, ALU.mult)
+        def page_of(m):
+            return pages[5 % PAGES] if m == 7 else pages[m % PAGES]
+
+        def scatter(m, h, factor):
+            nc.vector.tensor_tensor(page_of(m)[:].indirect(place[:]), h[:], factor, ALU.mult)
 
         h_first = sb("h0", [P, S], F32, tag="h", bufs=3)
         for s in range(2):
             cols = slice(HALF * s, HALF * (s + 1))
             first_stage_half(0, s, h_first)
-            nc.scalar.activation(h_first[:, cols], h_first[:, cols], ACT.Copy, scale=gain_of(0))
             nc.vector.tensor_tensor(
-                pages[0][:].indirect(place[:, 32 * s : 32 * (s + 1)]), h_first[:, cols], wgs_rows[:, cols], ALU.mult
+                pages[0][:].indirect(place[:, 32 * s : 32 * (s + 1)]), h_first[:, cols], weights[0][:, cols], ALU.mult
             )
             if s == 0:
                 stationary[1] = quantize_natural(1)
 
-        turned = [sb("turned%d" % c, [P, 4, 512], BF16) for c in range(CHUNKS)]
+        def summed_turned(m, c, old_part):
+            page = pages[m % PAGES]
+            pair = 3 if (m == 5 and c >= 2) else (m + 2 - c // 2) % 3
+            acc = bank(2 * pair + c % 2, "fwd%d_%d" % (m, c))
+            for step, source in enumerate((old_part, page)):
+                for b in range(4):
+                    t0 = BANK * c + P * b
+                    nc.tensor.matmul(
+                        acc[:, P * b : P * (b + 1)],
+                        lhsT=source[:, t0 : t0 + P],
+                        rhs=ident[:],
+                        is_transpose=True,
+                        start=(step == 0 and b == 0),
+                        stop=(step == 1 and b == 3),
+                    )
+            return acc
 
         def difference_turned(m):
-            page = pages[m % PAGES]
             for c in range(CHUNKS):
-                acc = bank(2 + c, "fwd%d_%d" % (m, c))
-                for step, source in enumerate((old_rows[m], page)):
-                    for b in range(4):
-                        t0 = BANK * c + P * b
-                        nc.tensor.matmul(
-                            acc[:, P * b : P * (b + 1)],
-                            lhsT=source[:, t0 : t0 + P],
-                            rhs=ident[:],
-                            is_transpose=True,
-                            start=(step == 0 and b == 0),
-                            stop=(step == 1 and b == 3),
-                        )
-                nc.scalar.activation(
-                    turned[c][:, :, P * m : P * (m + 1)], acc[:].rearrange("p (b r) -> p b r", b=4), ACT.Abs
-                )
+                acc = summed_turned(m, c, old_rows[m])
+                src = acc[:].rearrange("p (b w u e) -> p u b w e", b=4, u=2, e=2)
+                for u in range(2):
+                    nc.scalar.activation(
+                        turned[c][:, :, u, 64 * m : 64 * (m + 1)].rearrange("p b (w e) -> p b w e", e=2),
+                        src[:, u],
+                        ACT.Abs,
+                    )
 
-        def quantize_z(g, c, z):
-            codes = sb("z_codes%d_%d" % (g, c), [P, BANK], U32)
-            plane = sb("z_plane%d_%d" % (g, c), [P, BANK], U8)
+        def difference_turned_low(e):
+            for c in range(CHUNKS):
+                acc = summed_turned(4 + e, c, old_low[:, e, :])
+                nc.scalar.activation(turned_low[c][:, e, :], acc[:], ACT.Abs)
+
+        def turn_back_low(c):
+            acc = bank((0, 1, 4, 5)[c], "back_low%d" % c, BF16, 2 * BANK)
+            for e in range(2):
+                for b in range(4):
+                    col = BANK * e + P * b
+                    nc.tensor.transpose(acc[:, col : col + P], turned_low[c][:, e, P * b : P * (b + 1)], ident_bf[:])
+            for k, (t0, width) in enumerate(PIECES):
+                if t0 // BANK == c:
+                    if k < 3:
+                        z = sb("z1_%d" % k, [P, 4 * width], BF16, tag="old_rows", bufs=3)
+                    else:
+                        z = sb("z1_%d" % k, [P, 4 * width], BF16, tag="grouped_dealt%d" % (k - 3))
+                    nc.scalar.copy(
+                        z[:].rearrange("p (t u e) -> p u t e", u=2, e=2)[:, 0],
+                        acc[:].rearrange("p (e t) -> p t e", e=2)[:, t0 % BANK : t0 % BANK + width],
+                    )
+                    z_second.append(z)
+
+        def quantize_z(g, c, z, width=BANK):
+            codes = sb("z_codes%d_%d" % (g, c), [P, width], U32)
+            plane = sb("z_plane%d_%d" % (g, c), [P, width], U8)
             nc.vector.quantize_mx(out=codes[:].bitcast(FP8X4), scales=plane[:], in_=z[:])
             return codes, plane
 
         def turn_back(c):
             z = sb("z0_%d" % c, [P, 4 * BANK], BF16, tag="z", bufs=4)
             for half in range(2):
-                acc = bank(6 + half, "back%d_%d" % (c, half))
+                acc = bank(2 * (2, 3, 1, 3)[c] + half, "back%d_%d" % (c, half))
                 for b in range(2):
-                    pairs = turned[c][:, 2 * half + b, :].bitcast(F32)
                     for u in range(2):
                         col = P * (2 * b + u)
-                        nc.tensor.transpose(acc[:, col : col + P], pairs[:, u:256:2], ident[:])
+                        pairs = turned[c][:, 2 * half + b, u, :].bitcast(F32)
+                        nc.tensor.transpose(acc[:, col : col + P], pairs, ident[:])
                 nc.scalar.copy(
                     z[:, 1024 * half : 1024 * (half + 1)].bitcast(F32).rearrange("p (b t u) -> p b t u", b=2, u=2),
                     acc[:].rearrange("p (b u t) -> p b t u", b=2, u=2),
@@ -214,17 +265,15 @@ def tile_list_replay_slot_priority_kernel(
 
         stationary[2] = quantize_natural(2)
         stationary[3] = quantize_natural(3)
+        turned = [sb("turned%d" % c, [P, 4, 2, 256], BF16) for c in range(CHUNKS)]
         h1 = first_stage(1)
-        scatter(1, h1, wgs_rows[:])
-        dealt0 = quantize_dealt(0)
+        scatter(1, h1, weights[1][:])
         h2 = first_stage(2)
-        scatter(2, h2, wgs_rows[:])
-        dealt1 = quantize_dealt(1)
-        for i in range(4):
-            stationary[4 + i] = [dealt0[i], dealt1[i]]
+        scatter(2, h2, weights[2][:])
+        quantize_dealt(0)
 
         wgs_dealt = sb("wgs_dealt", [P, 4, S], F32, tag="big1")
-        for q in range(4):
+        for q in (0, 2, 1, 3):
             nc.sync.dma_start(wgs_dealt[32 * q : 32 * (q + 1)], wgs.rearrange("(m i) s -> m i s", i=4))
         old_rows.append(load_old_rows(3))
         old_dealt = old[512:1024, :].rearrange("(p u e) t -> u p e t", u=2, e=2)
@@ -238,69 +287,68 @@ def tile_list_replay_slot_priority_kernel(
                 w2_scales[:, 4 * q : 4 * q + 4, :].rearrange("a r c -> r a c").bitcast(I32),
             )
         old_high = []
-        for c in range(CHUNKS):
-            piece = sb("old_high%d" % c, [P, 2, BANK], F32)
-            nc.sync.dma_start(piece[:], old_dealt[1][:, :, BANK * c : BANK * (c + 1)])
+        for k, (t0, width) in enumerate(PIECES):
+            piece = sb("old_high%d" % k, [P, 2, width], F32)
+            nc.sync.dma_start(piece[:], old_dealt[1][:, :, t0 : t0 + width])
             old_high.append(piece)
 
         difference_turned(0)
         h3 = first_stage(3)
-        scatter(3, h3, wgs_rows[:])
+        scatter(3, h3, weights[3][:])
         difference_turned(1)
         h4 = first_stage(4)
         scatter(4, h4, wgs_dealt[:, 0, :])
-        nc.vector.tensor_tensor(old_low[:, 0, :], old_low[:, 0, :], pages[4 % PAGES][:], ALU.add)
+        quantize_dealt(1)
         difference_turned(2)
         h5 = first_stage(5)
         scatter(5, h5, wgs_dealt[:, 1, :])
-        nc.vector.tensor_tensor(old_low[:, 1, :], old_low[:, 1, :], pages[5 % PAGES][:], ALU.add)
-        h6 = first_stage(6)
         difference_turned(3)
+        h6 = first_stage(6)
         scatter(6, h6, wgs_dealt[:, 2, :])
-        for c in range(CHUNKS):
-            cols = slice(BANK * c, BANK * (c + 1))
-            nc.vector.tensor_tensor(old_high[c][:, 0, :], old_high[c][:, 0, :], pages[6 % PAGES][:, cols], ALU.add)
-        h7 = first_stage(7)
+        for k, (t0, width) in enumerate(PIECES):
+            nc.vector.tensor_tensor(old_high[k][:, 0, :], old_high[k][:, 0, :], page_of(6)[:, t0 : t0 + width], ALU.add)
         z_first = [turn_back(c) for c in range(CHUNKS)]
+        h7 = first_stage(7)
+        turned_low = [sb("turned_low%d" % c, [P, 2, BANK], BF16, tag="turned%d" % c) for c in range(CHUNKS)]
+        difference_turned_low(0)
+        difference_turned_low(1)
         scatter(7, h7, wgs_dealt[:, 3, :])
-
-        def second_pass(acc, g, n, z):
-            codes, plane = z
-            nc.tensor.matmul_mx(
-                out=acc[:],
-                lhsT=w2_codes[:, g, 2 * P * n : 2 * P * (n + 1)].bitcast(FP4X4),
-                lhsT_scale=w2_plane[:, g, P * n : P * (n + 1)],
-                rhs=codes[:].bitcast(FP8X4),
-                rhs_scale=plane[:],
-                start=(g == 0),
-                stop=(g == 1),
-            )
-
-        def absolute_pair(z, u, pair):
-            nc.scalar.activation(
-                z[:].rearrange("p (t u e) -> p u t e", u=2, e=2)[:, u], pair.rearrange("p e t -> p t e"), ACT.Abs
-            )
-
-        sums = {}
         z_second = []
         for c in range(CHUNKS):
-            for n in range(2):
-                sums[c, n] = bank((2 + 2 * c + n) % 8, "sum%d_%d" % (c, n))
-                second_pass(sums[c, n], 0, n, z_first[c])
-            z = sb("z1_%d" % c, [P, 4 * BANK], BF16, tag="z", bufs=4)
-            absolute_pair(z, 0, old_low[:, :, BANK * c : BANK * (c + 1)])
-            z_second.append(z)
+            turn_back_low(c)
 
-        staged = [sb("staged%d" % n, [P, CHUNKS, BANK], F32, tag="mid%d" % n) for n in range(2)]
-        for c in range(CHUNKS):
-            cols = slice(BANK * c, BANK * (c + 1))
-            nc.vector.tensor_tensor(old_high[c][:, 1, :], old_high[c][:, 1, :], pages[7 % PAGES][:, cols], ALU.add)
-            absolute_pair(z_second[c], 1, old_high[c][:])
-            z = quantize_z(1, c, z_second[c])
+        def second_passes(acc, g, n, codes, plane, width):
+            run = BANK if width == BANK else P
+            for c0 in range(0, width, run):
+                nc.tensor.matmul_mx(
+                    out=acc[:, c0 : c0 + run],
+                    lhsT=w2_codes[:, g, 2 * P * n : 2 * P * (n + 1)].bitcast(FP4X4),
+                    lhsT_scale=w2_plane[:, g, P * n : P * (n + 1)],
+                    rhs=codes[:, c0 : c0 + run].bitcast(FP8X4),
+                    rhs_scale=plane[:, c0 : c0 + run],
+                    start=(g == 0 and c0 == 0),
+                    stop=(g == 1 and c0 + run == width),
+                )
+
+        staged = [sb("staged%d" % n, [P, T2], F32, tag="mid%d" % n) for n in range(2)]
+        for k, (t0, width) in enumerate(PIECES):
+            cols = slice(t0, t0 + width)
+            nc.vector.tensor_tensor(old_high[k][:, 1, :], old_high[k][:, 1, :], page_of(7)[:, cols], ALU.add)
+            nc.scalar.activation(
+                z_second[k][:].rearrange("p (t u e) -> p u t e", u=2, e=2)[:, 1],
+                old_high[k][:].rearrange("p e t -> p t e"),
+                ACT.Abs,
+            )
+            codes, plane = quantize_z(1, k, z_second[k], width)
+            first_codes, first_plane = z_first[t0 // BANK]
+            there = slice(t0 % BANK, t0 % BANK + width)
+            sums = [bank(2 * (k % 4) + n, "sum%d_%d" % (k, n)) for n in range(2)]
             for n in range(2):
-                second_pass(sums[c, n], 1, n, z)
-                if n == 1 and c >= 2:
-                    nc.scalar.copy(staged[n][:, c, :], sums[c, n][:])
+                second_passes(sums[n], 0, n, first_codes[:, there], first_plane[:, there], width)
+            for n in range(2):
+                second_passes(sums[n], 1, n, codes[:], plane[:], width)
+                if n == 1 and k >= 2:
+                    nc.scalar.copy(staged[n][:, cols], sums[n][:, 0:width])
                 else:
-                    nc.vector.tensor_copy(staged[n][:, c, :], sums[c, n][:])
-                nc.sync.dma_start(out[P * n : P * (n + 1), cols], staged[n][:, c, :])
+                    nc.vector.tensor_copy(staged[n][:, cols], sums[n][:, 0:width])
+                nc.sync.dma_start(out[P * n : P * (n + 1), cols], staged[n][:, cols])

@@ -17,11 +17,25 @@ FP4X4 = mybir.dt.float4_e2m1fn_x4
 ACT = mybir.ActivationFunctionType
 ALU = mybir.AluOpType
 
+KIB = 1024
 BANK = 512
 HALF = S // 2
+QUARTER = S // 4
 CHUNKS = T2 // BANK
 PAGES = 3
-PIECES = [(0, 512), (512, 512), (1024, 512), (1536, 256), (1792, 256)]
+H_SLOTS = 5
+PIECES = [(0, 256), (256, 512), (768, 512), (1280, 512), (1792, 256)]
+
+WORDS0 = 0
+WORDS1 = 16 * KIB
+RAW_NATURAL = 32 * KIB
+PAIR_WORDS = 33 * KIB
+RAW_DEALT = 49 * KIB
+GROUPED_NATURAL = 65 * KIB
+WGS_DEALT = 69 * KIB
+OLD_ROWS = 81 * KIB
+H_RING = 113 * KIB
+GROUPED_DEALT = H_RING + 4 * KIB * H_SLOTS
 
 
 def tile_list_replay_slot_priority_kernel(
@@ -30,13 +44,17 @@ def tile_list_replay_slot_priority_kernel(
     nc = tc.nc
     with ExitStack() as ctx:
         keep = ctx.enter_context(tc.tile_pool(name="keep", bufs=1))
+        shared = ctx.enter_context(tc.tile_pool(name="shared", bufs=1))
         psum = ctx.enter_context(tc.psum_pool(name="psum", bufs=1))
 
         def sb(name, shape, dtype, tag=None, bufs=1):
             return keep.tile(shape, dtype, name=name, tag=tag or name, bufs=bufs, align_bytes=64)
 
-        def bank(b, name, dtype=F32, width=BANK):
-            return psum.tile([P, width], dtype, name=name, tag="bank%d" % b)
+        def at(offset, name, shape, dtype):
+            return shared.tile(shape, dtype, name=name, offset=offset, align_bytes=64)
+
+        def bank(b, name):
+            return psum.tile([P, BANK], F32, name=name, tag="bank%d" % b)
 
         tab_plane = sb("tab_plane", [P, T], U8)
         nc.vector.memset(tab_plane[:, 0 : T // 2].bitcast(I32), 0)
@@ -51,68 +69,74 @@ def tile_list_replay_slot_priority_kernel(
         nc.sync.dma_start(gain_dealt[:], gain[512:1024].rearrange("(p i) -> p i", i=4))
         nc.sync.dma_start(gain_flat[0:4, :], gain[0:512].rearrange("(m p) -> m p", p=P))
 
+        def load_w1(offset, name, a, c0, width, parts=1):
+            raw = at(offset, name, [P, 4, width], F32)
+            rows = w1[512 * a : 512 * (a + 1), c0 : c0 + width].rearrange("(p j) c -> p j c", j=4)
+            for part in range(parts):
+                js = slice(4 * part // parts, 4 * (part + 1) // parts)
+                nc.sync.dma_start(raw[:, js, :], rows[:, js, :])
+            return raw
 
-        words = [sb("words%d" % a, [P, T], U32, tag="big%d" % a) for a in range(2)]
+        raw_first = [load_w1(RAW_NATURAL + 2 * KIB * a, "raw_first%d" % a, a, 0, 128, 2) for a in range(2)]
+        words = [at(offset, "words%d" % a, [P, T], U32) for a, offset in enumerate((WORDS0, WORDS1))]
 
         def load_words(a, cols):
             nc.sync.dma_start(
                 words[a][:, cols].bitcast(I32), tab_words[a].rearrange("p t i -> p (t i)").bitcast(I32)[:, cols]
             )
 
-        def load_w1(name, a, c0, width, tag=None):
-            raw = sb(name, [P, 4, width], F32, tag=tag)
-            nc.sync.dma_start(
-                raw[:], w1[512 * a : 512 * (a + 1), c0 : c0 + width].rearrange("(p j) c -> p j c", j=4)
-            )
-            return raw
-
         for piece in range(4):
             load_words(0, slice(piece * T // 4, (piece + 1) * T // 4))
-        raw_first = [load_w1("raw_first%d" % a, a, 0, 128) for a in range(2)]
-        wgs_rows = sb("wgs_rows", [P, S], F32)
-        nc.sync.dma_start(wgs_rows[:], wgs)
         for q in range(4):
             nc.sync.dma_start(
                 tab_plane[32 * q : 32 * q + 8, :].bitcast(I32),
                 tab_scales[:, 4 * q : 4 * q + 4, :].bitcast(I32),
             )
         load_words(1, slice(0, T))
-        raw_second = [load_w1("raw_second%d" % a, a, 128, 128) for a in range(2)]
-        raw_third = [load_w1("raw_third%d" % a, a, 256, 256, tag="turned%d" % a) for a in range(2)]
-        raw_dealt = [load_w1("raw_dealt%d" % a, a, 512, 512, tag="mid%d" % a) for a in range(2)]
+        wgs_rows = sb("wgs_rows", [P, S], F32)
+        nc.sync.dma_start(wgs_rows[:], wgs)
+        raw_second = [load_w1(RAW_NATURAL + 4 * KIB + 2 * KIB * a, "raw_second%d" % a, a, 128, 128) for a in range(2)]
+        raw_third = [load_w1(RAW_NATURAL + 8 * KIB + 4 * KIB * a, "raw_third%d" % a, a, 256, 256) for a in range(2)]
+
+        def load_old_rows(m):
+            rows = at(OLD_ROWS + 8 * KIB * m, "old_rows%d" % m, [P, T2], F32)
+            nc.sync.dma_start(rows[:], old[P * m : P * (m + 1), :])
+            return rows
+
+        old_rows = [load_old_rows(0)]
+        raw_dealt = [load_w1(RAW_DEALT + 8 * KIB * a, "raw_dealt%d" % a, a, 512, 512) for a in range(2)]
+        old_rows.append(load_old_rows(1))
+        wgs_planes = wgs.rearrange("(m i) s -> m i s", i=4)
+        wgs_dealt = at(WGS_DEALT, "wgs_dealt", [P, 3, S], F32)
+        for q in (0, 2, 1, 3):
+            nc.sync.dma_start(wgs_dealt[32 * q : 32 * (q + 1)], wgs_planes[:, 0:3, :])
+        old_rows.append(load_old_rows(2))
+        old_rows.append(load_old_rows(3))
+        wgs_last = sb("wgs_last", [P, S], F32)
+        for q in (0, 2, 1, 3):
+            nc.sync.dma_start(wgs_last[32 * q : 32 * (q + 1)], wgs_planes[:, 3, :])
 
         pages = [sb("page%d" % i, [P, T2], F32) for i in range(PAGES)]
         for page in pages[:2]:
             nc.vector.memset(page[:], 0.0)
         ident = sb("ident", [P, P], F32)
         make_identity(nc, ident[:])
-        ident_bf = sb("ident_bf", [P, P], BF16)
-        make_identity(nc, ident_bf[:])
-        for page in pages[2:]:
-            nc.gpsimd.memset(page[:], 0.0)
+        nc.gpsimd.memset(pages[2][:], 0.0)
         gain_rows = sb("gain_rows", [P, 4], F32)
-        gain_bank = bank(6, "gain_bank")
+        gain_bank = bank(7, "gain_bank")
         nc.tensor.transpose(gain_bank[:, 0:P], gain_flat[:], ident[:])
         nc.scalar.copy(gain_rows[:], gain_bank[:, 0:4])
         w2_plane = sb("w2_plane", [P, 2, N], U8)
         nc.vector.memset(w2_plane[:].rearrange("p a c -> p (a c)").bitcast(I32), 0)
 
-        def load_old_rows(m):
-            rows = sb("old_rows%d" % m, [P, T2], F32, tag="old_rows", bufs=3)
-            nc.sync.dma_start(rows[:], old[P * m : P * (m + 1), :])
-            return rows
-
-        old_rows = [load_old_rows(m) for m in range(3)]
-
         v0 = sb("v0", [P, S], U32)
         v1 = [sb("v1_%d" % s, [P, HALF], U32) for s in range(2)]
         v_plane = sb("v_plane", [P, S], U8)
-        nc.vector.tensor_copy(v0[:], words[0][:].indirect(pick[:]))
-        nc.vector.tensor_copy(v_plane[:], tab_plane[:].indirect(pick[:]))
+        stationary = {}
 
         def quantize_natural(m):
             raw, c0 = ((raw_first, 0), (raw_second, 0), (raw_third, 0), (raw_third, P))[m]
-            grouped = sb("grouped%d" % m, [P, 2, P * 4], BF16, tag="grouped", bufs=2)
+            grouped = at(GROUPED_NATURAL + 2 * KIB * (m % 2), "grouped%d" % m, [P, 2, P * 4], BF16)
             for a in range(2):
                 nc.scalar.copy(
                     grouped[:, a, :].rearrange("p (c i j) -> p c j i", i=4, j=4),
@@ -123,10 +147,10 @@ def tile_list_replay_slot_priority_kernel(
             nc.vector.quantize_mx(
                 out=codes[:].bitcast(FP8X4), scales=plane[:], in_=grouped[:].rearrange("p a c -> p (a c)")
             )
-            return [(codes[:, P * a : P * (a + 1)], plane[:, P * a : P * (a + 1)]) for a in range(2)]
+            stationary[m] = [(codes[:, P * a : P * (a + 1)], plane[:, P * a : P * (a + 1)]) for a in range(2)]
 
         def quantize_dealt(u):
-            grouped = sb("grouped_dealt%d" % u, [P, 2, 1024], BF16)
+            grouped = at(GROUPED_DEALT + 4 * KIB * u, "grouped_dealt%d" % u, [P, 2, 1024], BF16)
             for a in range(2):
                 nc.scalar.copy(
                     grouped[:, a, :].rearrange("p (e m j) -> p m j e", e=2, j=4),
@@ -141,23 +165,31 @@ def tile_list_replay_slot_priority_kernel(
                 spans = [slice(P * (2 * a + e), P * (2 * a + e + 1)) for a in range(2)]
                 stationary[4 + 2 * u + e] = [(codes[:, span], plane[:, span]) for span in spans]
 
-        stationary = {0: quantize_natural(0)}
-        weights = []
-        for m in range(4):
-            scaled = sb("weights%d" % m, [P, S], F32, tag="z", bufs=4)
-            nc.vector.tensor_scalar_mul(scaled[:], wgs_rows[:], gain_rows[:, m : m + 1])
-            weights.append(scaled)
+        quantize_natural(0)
+        nc.vector.tensor_copy(v0[:], words[0][:].indirect(pick[:]))
+        nc.vector.tensor_copy(v_plane[:], tab_plane[:].indirect(pick[:]))
         for s in range(2):
             nc.vector.tensor_copy(v1[s][:], words[1][:].indirect(pick[:, 32 * s : 32 * (s + 1)]))
 
-        def first_stage_half(m, s, h):
-            acc = bank(2 * (m % 3) + s, "acc%d_%d" % (m, s))
-            cols = slice(HALF * s, HALF * (s + 1))
+        old_dealt = old[512:1024, :].rearrange("(p u e) t -> u p e t", u=2, e=2)
+        for q in range(4):
+            nc.sync.dma_start(
+                w2_plane[32 * q : 32 * q + 4].bitcast(I32),
+                w2_scales[:, 4 * q : 4 * q + 4, :].rearrange("a r c -> r a c").bitcast(I32),
+            )
+        old_low = at(WORDS0, "old_low", [P, 2, T2], F32)
+        nc.sync.dma_start(old_low[:], old_dealt[0])
+        old_high = at(WORDS1, "old_high", [P, 2, T2], F32)
+        nc.sync.dma_start(old_high[:], old_dealt[1])
+
+        def first_stage_part(m, h, c0, width, b):
+            acc = bank(b, "acc%d_%d" % (m, c0))
+            cols = slice(c0, c0 + width)
             for a in range(2):
                 codes, plane = stationary[m][a]
-                moving = v0[:, cols] if a == 0 else v1[s][:]
+                moving = v0[:, cols] if a == 0 else v1[c0 // HALF][:, c0 % HALF : c0 % HALF + width]
                 nc.tensor.matmul_mx(
-                    out=acc[:],
+                    out=acc[:, 0:width],
                     lhsT=codes.bitcast(FP8X4),
                     lhsT_scale=plane,
                     rhs=moving.bitcast(FP8X4),
@@ -165,52 +197,70 @@ def tile_list_replay_slot_priority_kernel(
                     start=(a == 0),
                     stop=(a == 1),
                 )
-            nc.scalar.activation(h[:, cols], acc[:], ACT.Tanh, scale=-1.0)
+            nc.scalar.activation(h[:, cols], acc[:, 0:width], ACT.Tanh, scale=-1.0)
 
-        def first_stage(m):
-            h = sb("h%d" % m, [P, S], F32, tag="h", bufs=3)
+        def h_tile(m):
+            return at(H_RING + 4 * KIB * (m % H_SLOTS), "h%d" % m, [P, S], F32)
+
+        def weights_of(m, cols):
+            scaled = sb("weights%d" % m, [P, S], F32, tag="weights", bufs=2)
+            nc.gpsimd.tensor_scalar(scaled[:, cols], wgs_rows[:, cols], gain_rows[:, m : m + 1], 0.0, ALU.mult, ALU.add)
+            return scaled
+
+        def weighted(m):
+            h = h_tile(m)
+            if m < 4:
+                factor = weights_of(m, slice(0, S))[:]
+            elif m < 7:
+                factor = wgs_dealt[:, m - 4, :]
+            else:
+                factor = wgs_last[:]
             for s in range(2):
-                first_stage_half(m, s, h)
+                first_stage_part(m, h, HALF * s, HALF, s + (6 if m == 7 else 0))
             if m >= 4:
                 nc.scalar.activation(h[:], h[:], ACT.Copy, scale=gain_dealt[:, m - 4 : m - 3])
+            nc.gpsimd.tensor_tensor(h[:], h[:], factor, ALU.mult)
             return h
 
         def page_of(m):
-            return pages[5 % PAGES] if m == 7 else pages[m % PAGES]
+            return pages[m % PAGES]
 
-        def scatter(m, h, factor):
-            nc.vector.tensor_tensor(page_of(m)[:].indirect(place[:]), h[:], factor, ALU.mult)
-
-        h_first = sb("h0", [P, S], F32, tag="h", bufs=3)
-        for s in range(2):
-            cols = slice(HALF * s, HALF * (s + 1))
-            first_stage_half(0, s, h_first)
-            nc.vector.tensor_tensor(
-                pages[0][:].indirect(place[:, 32 * s : 32 * (s + 1)]), h_first[:, cols], weights[0][:, cols], ALU.mult
+        def scatter(m, h, c0=0, width=S):
+            nc.vector.tensor_copy(
+                page_of(m)[:].indirect(place[:, c0 // 16 : (c0 + width) // 16]), h[:, c0 : c0 + width]
             )
-            if s == 0:
-                stationary[1] = quantize_natural(1)
 
-        def summed_turned(m, c, old_part):
-            page = pages[m % PAGES]
-            pair = 3 if (m == 5 and c >= 2) else (m + 2 - c // 2) % 3
-            acc = bank(2 * pair + c % 2, "fwd%d_%d" % (m, c))
-            for step, source in enumerate((old_part, page)):
-                for b in range(4):
-                    t0 = BANK * c + P * b
-                    nc.tensor.matmul(
-                        acc[:, P * b : P * (b + 1)],
-                        lhsT=source[:, t0 : t0 + P],
-                        rhs=ident[:],
-                        is_transpose=True,
-                        start=(step == 0 and b == 0),
-                        stop=(step == 1 and b == 3),
-                    )
-            return acc
+        h_first = h_tile(0)
+        weights_first = weights_of(0, slice(QUARTER, S))
+        for c0, width, b in ((0, QUARTER, 0), (QUARTER, QUARTER, 6), (HALF, HALF, 1)):
+            cols = slice(c0, c0 + width)
+            first_stage_part(0, h_first, c0, width, b)
+            if c0 == 0:
+                nc.vector.scalar_tensor_tensor(
+                    h_first[:, cols], h_first[:, cols], gain_rows[:, 0:1], wgs_rows[:, cols], ALU.mult, ALU.mult
+                )
+            else:
+                nc.gpsimd.tensor_tensor(h_first[:, cols], h_first[:, cols], weights_first[:, cols], ALU.mult)
+            scatter(0, h_first, c0, width)
+            if c0 == 0:
+                quantize_natural(1)
+
+        turned = [at(RAW_NATURAL + 4 * KIB * ((c + 1) % CHUNKS), "turned%d" % c, [P, 4, 2, 256], BF16) for c in range(CHUNKS)]
 
         def difference_turned(m):
             for c in range(CHUNKS):
-                acc = summed_turned(m, c, old_rows[m])
+                acc = bank(2 + c, "fwd%d_%d" % (m, c))
+                for step, source in enumerate((old_rows[m], pages[m % PAGES])):
+                    for b in range(4):
+                        t0 = BANK * c + P * b
+                        nc.tensor.matmul(
+                            acc[:, P * b : P * (b + 1)],
+                            lhsT=source[:, t0 : t0 + P],
+                            rhs=ident[:],
+                            is_transpose=True,
+                            start=(step == 0 and b == 0),
+                            stop=(step == 1 and b == 3),
+                        )
                 src = acc[:].rearrange("p (b w u e) -> p u b w e", b=4, u=2, e=2)
                 for u in range(2):
                     nc.scalar.activation(
@@ -219,136 +269,124 @@ def tile_list_replay_slot_priority_kernel(
                         ACT.Abs,
                     )
 
-        def difference_turned_low(e):
-            for c in range(CHUNKS):
-                acc = summed_turned(4 + e, c, old_low[:, e, :])
-                nc.scalar.activation(turned_low[c][:, e, :], acc[:], ACT.Abs)
+        h_next = weighted(1)
+        quantize_natural(2)
+        quantize_natural(3)
+        scatter(1, h_next)
+        h_next = weighted(2)
+        quantize_dealt(0)
+        difference_turned(0)
+        scatter(2, h_next)
+        h_next = weighted(3)
+        quantize_dealt(1)
+        difference_turned(1)
+        scatter(3, h_next)
+        h_dealt = [weighted(4), weighted(5)]
+        difference_turned(2)
+        scatter(4, h_dealt[0])
+        h_dealt.append(weighted(6))
+        difference_turned(3)
+        scatter(5, h_dealt[1])
 
-        def turn_back_low(c):
-            acc = bank((0, 1, 4, 5)[c], "back_low%d" % c, BF16, 2 * BANK)
-            for e in range(2):
-                for b in range(4):
-                    col = BANK * e + P * b
-                    nc.tensor.transpose(acc[:, col : col + P], turned_low[c][:, e, P * b : P * (b + 1)], ident_bf[:])
-            for k, (t0, width) in enumerate(PIECES):
-                if t0 // BANK == c:
-                    if k < 3:
-                        z = sb("z1_%d" % k, [P, 4 * width], BF16, tag="old_rows", bufs=3)
-                    else:
-                        z = sb("z1_%d" % k, [P, 4 * width], BF16, tag="grouped_dealt%d" % (k - 3))
-                    nc.scalar.copy(
-                        z[:].rearrange("p (t u e) -> p u t e", u=2, e=2)[:, 0],
-                        acc[:].rearrange("p (e t) -> p t e", e=2)[:, t0 % BANK : t0 % BANK + width],
-                    )
-                    z_second.append(z)
+        low = at(GROUPED_NATURAL, "low", [P, 2, T2], F32)
 
-        def quantize_z(g, c, z, width=BANK):
-            codes = sb("z_codes%d_%d" % (g, c), [P, width], U32)
-            plane = sb("z_plane%d_%d" % (g, c), [P, width], U8)
-            nc.vector.quantize_mx(out=codes[:].bitcast(FP8X4), scales=plane[:], in_=z[:])
-            return codes, plane
-
-        def turn_back(c):
-            z = sb("z0_%d" % c, [P, 4 * BANK], BF16, tag="z", bufs=4)
+        def sum_low(e):
             for half in range(2):
-                acc = bank(2 * (2, 3, 1, 3)[c] + half, "back%d_%d" % (c, half))
+                cols = slice(1024 * half, 1024 * (half + 1))
+                nc.gpsimd.tensor_tensor(low[:, e, cols], old_low[:, e, cols], pages[(4 + e) % PAGES][:, cols], ALU.add)
+
+        sum_low(0)
+        z_first = [at(RAW_DEALT + 8 * KIB * g, "z_first%d" % g, [P, 4096], BF16) for g in range(2)]
+        for c in range(CHUNKS):
+            for half in range(2):
+                acc = bank((6, 2, 4, 6)[c] + half, "back%d_%d" % (c, half))
                 for b in range(2):
                     for u in range(2):
                         col = P * (2 * b + u)
                         pairs = turned[c][:, 2 * half + b, u, :].bitcast(F32)
                         nc.tensor.transpose(acc[:, col : col + P], pairs, ident[:])
+                z0 = 2048 * (c % 2) + 1024 * half
                 nc.scalar.copy(
-                    z[:, 1024 * half : 1024 * (half + 1)].bitcast(F32).rearrange("p (b t u) -> p b t u", b=2, u=2),
+                    z_first[c // 2][:, z0 : z0 + 1024].bitcast(F32).rearrange("p (b t u) -> p b t u", b=2, u=2),
                     acc[:].rearrange("p (b u t) -> p b t u", b=2, u=2),
                 )
-            return quantize_z(0, c, z)
-
-        stationary[2] = quantize_natural(2)
-        stationary[3] = quantize_natural(3)
-        turned = [sb("turned%d" % c, [P, 4, 2, 256], BF16) for c in range(CHUNKS)]
-        h1 = first_stage(1)
-        scatter(1, h1, weights[1][:])
-        h2 = first_stage(2)
-        scatter(2, h2, weights[2][:])
-        quantize_dealt(0)
-
-        wgs_dealt = sb("wgs_dealt", [P, 4, S], F32, tag="big1")
-        for q in (0, 2, 1, 3):
-            nc.sync.dma_start(wgs_dealt[32 * q : 32 * (q + 1)], wgs.rearrange("(m i) s -> m i s", i=4))
-        old_rows.append(load_old_rows(3))
-        old_dealt = old[512:1024, :].rearrange("(p u e) t -> u p e t", u=2, e=2)
-        old_low = sb("old_low", [P, 2, T2], F32, tag="big0")
-        nc.sync.dma_start(old_low[:], old_dealt[0])
-        w2_codes = sb("w2_codes", [P, 2, 2 * N], U8)
+        w2_codes = at(RAW_NATURAL, "w2_codes", [P, 2, 2 * N], U8)
         nc.sync.dma_start(w2_codes[:].bitcast(I32), w2_words.rearrange("a p c -> p a c").bitcast(I32))
-        for q in range(4):
-            nc.sync.dma_start(
-                w2_plane[32 * q : 32 * q + 4].bitcast(I32),
-                w2_scales[:, 4 * q : 4 * q + 4, :].rearrange("a r c -> r a c").bitcast(I32),
+        scatter(6, h_dealt[2])
+        sum_low(1)
+        h_last = weighted(7)
+        first_codes = sb("first_codes", [P, T2], U32)
+        first_plane = sb("first_plane", [P, T2], U8)
+        for g in range(2):
+            cols = slice(1024 * g, 1024 * (g + 1))
+            nc.vector.quantize_mx(out=first_codes[:, cols].bitcast(FP8X4), scales=first_plane[:, cols], in_=z_first[g][:])
+        scatter(7, h_last)
+
+        def second_pass(acc, g, n, codes, plane, start, stop):
+            nc.tensor.matmul_mx(
+                out=acc,
+                lhsT=w2_codes[:, g, 2 * P * n : 2 * P * (n + 1)].bitcast(FP4X4),
+                lhsT_scale=w2_plane[:, g, P * n : P * (n + 1)],
+                rhs=codes.bitcast(FP8X4),
+                rhs_scale=plane,
+                start=start,
+                stop=stop,
             )
-        old_high = []
-        for k, (t0, width) in enumerate(PIECES):
-            piece = sb("old_high%d" % k, [P, 2, width], F32)
-            nc.sync.dma_start(piece[:], old_dealt[1][:, :, t0 : t0 + width])
-            old_high.append(piece)
 
-        difference_turned(0)
-        h3 = first_stage(3)
-        scatter(3, h3, weights[3][:])
-        difference_turned(1)
-        h4 = first_stage(4)
-        scatter(4, h4, wgs_dealt[:, 0, :])
-        quantize_dealt(1)
-        difference_turned(2)
-        h5 = first_stage(5)
-        scatter(5, h5, wgs_dealt[:, 1, :])
-        difference_turned(3)
-        h6 = first_stage(6)
-        scatter(6, h6, wgs_dealt[:, 2, :])
-        for k, (t0, width) in enumerate(PIECES):
-            nc.vector.tensor_tensor(old_high[k][:, 0, :], old_high[k][:, 0, :], page_of(6)[:, t0 : t0 + width], ALU.add)
-        z_first = [turn_back(c) for c in range(CHUNKS)]
-        h7 = first_stage(7)
-        turned_low = [sb("turned_low%d" % c, [P, 2, BANK], BF16, tag="turned%d" % c) for c in range(CHUNKS)]
-        difference_turned_low(0)
-        difference_turned_low(1)
-        scatter(7, h7, wgs_dealt[:, 3, :])
-        z_second = []
-        for c in range(CHUNKS):
-            turn_back_low(c)
-
-        def second_passes(acc, g, n, codes, plane, width):
-            run = BANK if width == BANK else P
-            for c0 in range(0, width, run):
-                nc.tensor.matmul_mx(
-                    out=acc[:, c0 : c0 + run],
-                    lhsT=w2_codes[:, g, 2 * P * n : 2 * P * (n + 1)].bitcast(FP4X4),
-                    lhsT_scale=w2_plane[:, g, P * n : P * (n + 1)],
-                    rhs=codes[:, c0 : c0 + run].bitcast(FP8X4),
-                    rhs_scale=plane[:, c0 : c0 + run],
-                    start=(g == 0 and c0 == 0),
-                    stop=(g == 1 and c0 + run == width),
-                )
-
-        staged = [sb("staged%d" % n, [P, T2], F32, tag="mid%d" % n) for n in range(2)]
+        high, pair_words, sums = [], [], []
+        next_bank = 0
         for k, (t0, width) in enumerate(PIECES):
             cols = slice(t0, t0 + width)
-            nc.vector.tensor_tensor(old_high[k][:, 1, :], old_high[k][:, 1, :], page_of(7)[:, cols], ALU.add)
+            piece = at(RAW_DEALT + 8 * t0, "high%d" % k, [P, 2, width], F32)
+            nc.gpsimd.tensor_tensor(piece[:, 0, :], old_high[:, 0, cols], pages[6 % PAGES][:, cols], ALU.add)
+            high.append(piece)
+            both = at(PAIR_WORDS + 8 * t0, "pair_words%d" % k, [P, 2, 2 * width], BF16)
             nc.scalar.activation(
-                z_second[k][:].rearrange("p (t u e) -> p u t e", u=2, e=2)[:, 1],
-                old_high[k][:].rearrange("p e t -> p t e"),
+                both[:, 0, :].rearrange("p (t e) -> p t e", e=2), low[:, :, cols].rearrange("p e t -> p t e"), ACT.Abs
+            )
+            pair_words.append(both)
+            wide = width == BANK
+            banks = [bank(next_bank + n, "sum%d_%d" % (k, n)) for n in range(2 if wide else 1)]
+            next_bank = next_bank + len(banks)
+            accs = [banks[n][:] if wide else banks[0][:, width * n : width * (n + 1)] for n in range(2)]
+            for n in range(2):
+                second_pass(accs[n], 0, n, first_codes[:, cols], first_plane[:, cols], wide or n == 0, False)
+            sums.append((banks, accs))
+
+        out_rows = out.rearrange("(n p) t -> p n t", p=P)
+        for k, (t0, width) in enumerate(PIECES):
+            cols = slice(t0, t0 + width)
+            wide = width == BANK
+            nc.vector.tensor_tensor(high[k][:, 1, :], old_high[:, 1, cols], page_of(7)[:, cols], ALU.add)
+            nc.scalar.activation(
+                pair_words[k][:, 1, :].rearrange("p (t e) -> p t e", e=2),
+                high[k][:].rearrange("p e t -> p t e"),
                 ACT.Abs,
             )
-            codes, plane = quantize_z(1, k, z_second[k], width)
-            first_codes, first_plane = z_first[t0 // BANK]
-            there = slice(t0 % BANK, t0 % BANK + width)
-            sums = [bank(2 * (k % 4) + n, "sum%d_%d" % (k, n)) for n in range(2)]
+            z = at(OLD_ROWS + 8 * t0, "z_second%d" % k, [P, 4 * width], BF16)
+            nc.vector.tensor_copy(
+                z[:].bitcast(I32).rearrange("p (t u) -> p t u", u=2),
+                pair_words[k][:].bitcast(I32).rearrange("p u t -> p t u"),
+            )
+            codes = sb("second_codes%d" % k, [P, width], U32)
+            plane = sb("second_plane%d" % k, [P, width], U8)
+            nc.vector.quantize_mx(out=codes[:].bitcast(FP8X4), scales=plane[:], in_=z[:])
+            banks, accs = sums[k]
             for n in range(2):
-                second_passes(sums[n], 0, n, first_codes[:, there], first_plane[:, there], width)
-            for n in range(2):
-                second_passes(sums[n], 1, n, codes[:], plane[:], width)
-                if n == 1 and k >= 2:
-                    nc.scalar.copy(staged[n][:, cols], sums[n][:, 0:width])
+                second_pass(accs[n], 1, n, codes[:], plane[:], False, wide or n == 1)
+
+        for k, (t0, width) in enumerate(PIECES):
+            cols = slice(t0, t0 + width)
+            wide = width == BANK
+            banks, accs = sums[k]
+            staged = at(WORDS0 + 8 * t0, "staged%d" % k, [P, 2, width], F32)
+            if wide:
+                for n in range(2):
+                    nc.scalar.copy(staged[:, n, :], accs[n])
+                    nc.sync.dma_start(out_rows[:, n, cols], staged[:, n, :])
+            else:
+                if k == 0:
+                    nc.scalar.copy(staged[:].rearrange("p n t -> p (n t)"), banks[0][:])
                 else:
-                    nc.vector.tensor_copy(staged[n][:, cols], sums[n][:, 0:width])
-                nc.sync.dma_start(out[P * n : P * (n + 1), cols], staged[n][:, cols])
+                    nc.vector.tensor_copy(staged[:].rearrange("p n t -> p (n t)"), banks[0][:])
+                nc.sync.dma_start(out_rows[:, :, cols], staged[:])

@@ -29,13 +29,15 @@ PIECES = [(0, 256), (256, 512), (768, 512), (1280, 512), (1792, 256)]
 WORDS0 = 0
 WORDS1 = 16 * KIB
 RAW_NATURAL = 32 * KIB
-PAIR_WORDS = 33 * KIB
-RAW_DEALT = 49 * KIB
-GROUPED_NATURAL = 65 * KIB
+H_LAST = 33 * KIB
+PAIR_WORDS = 37 * KIB
+RAW_DEALT = 53 * KIB
 WGS_DEALT = 69 * KIB
-OLD_ROWS = 81 * KIB
-H_RING = 113 * KIB
+OLD_ROWS = 85 * KIB
+WEIGHTS = 117 * KIB
+H_RING = 133 * KIB
 GROUPED_DEALT = H_RING + 4 * KIB * H_SLOTS
+GROUPED_NATURAL = GROUPED_DEALT + 8 * KIB
 
 
 def tile_list_replay_slot_priority_kernel(
@@ -87,34 +89,31 @@ def tile_list_replay_slot_priority_kernel(
 
         for piece in range(4):
             load_words(0, slice(piece * T // 4, (piece + 1) * T // 4))
+        wgs_rows = sb("wgs_rows", [P, S], F32)
+        nc.sync.dma_start(wgs_rows[:], wgs)
         for q in range(4):
             nc.sync.dma_start(
                 tab_plane[32 * q : 32 * q + 8, :].bitcast(I32),
                 tab_scales[:, 4 * q : 4 * q + 4, :].bitcast(I32),
             )
         load_words(1, slice(0, T))
-        wgs_rows = sb("wgs_rows", [P, S], F32)
-        nc.sync.dma_start(wgs_rows[:], wgs)
-        raw_second = [load_w1(RAW_NATURAL + 4 * KIB + 2 * KIB * a, "raw_second%d" % a, a, 128, 128) for a in range(2)]
-        raw_third = [load_w1(RAW_NATURAL + 8 * KIB + 4 * KIB * a, "raw_third%d" % a, a, 256, 256) for a in range(2)]
+        raw_second = [load_w1(RAW_NATURAL + 4 * KIB + 4 * KIB * a, "raw_second%d" % a, a, 128, 256) for a in range(2)]
+        raw_third = [load_w1(RAW_NATURAL + 12 * KIB + 2 * KIB * a, "raw_third%d" % a, a, 384, 128) for a in range(2)]
 
         def load_old_rows(m):
             rows = at(OLD_ROWS + 8 * KIB * m, "old_rows%d" % m, [P, T2], F32)
             nc.sync.dma_start(rows[:], old[P * m : P * (m + 1), :])
             return rows
 
-        old_rows = [load_old_rows(0)]
         raw_dealt = [load_w1(RAW_DEALT + 8 * KIB * a, "raw_dealt%d" % a, a, 512, 512) for a in range(2)]
+        old_rows = [load_old_rows(0)]
         old_rows.append(load_old_rows(1))
         wgs_planes = wgs.rearrange("(m i) s -> m i s", i=4)
-        wgs_dealt = at(WGS_DEALT, "wgs_dealt", [P, 3, S], F32)
+        wgs_dealt = at(WGS_DEALT, "wgs_dealt", [P, 4, S], F32)
         for q in (0, 2, 1, 3):
-            nc.sync.dma_start(wgs_dealt[32 * q : 32 * (q + 1)], wgs_planes[:, 0:3, :])
+            nc.sync.dma_start(wgs_dealt[32 * q : 32 * (q + 1)], wgs_planes)
         old_rows.append(load_old_rows(2))
         old_rows.append(load_old_rows(3))
-        wgs_last = sb("wgs_last", [P, S], F32)
-        for q in (0, 2, 1, 3):
-            nc.sync.dma_start(wgs_last[32 * q : 32 * (q + 1)], wgs_planes[:, 3, :])
 
         pages = [sb("page%d" % i, [P, T2], F32) for i in range(PAGES)]
         for page in pages[:2]:
@@ -134,20 +133,22 @@ def tile_list_replay_slot_priority_kernel(
         v_plane = sb("v_plane", [P, S], U8)
         stationary = {}
 
-        def quantize_natural(m):
-            raw, c0 = ((raw_first, 0), (raw_second, 0), (raw_third, 0), (raw_third, P))[m]
-            grouped = at(GROUPED_NATURAL + 2 * KIB * (m % 2), "grouped%d" % m, [P, 2, P * 4], BF16)
+        def quantize_natural(m, raw, offset):
+            width = raw[0].shape[2]
+            grouped = at(offset, "grouped%d" % m, [P, 2, width * 4], BF16)
             for a in range(2):
                 nc.scalar.copy(
                     grouped[:, a, :].rearrange("p (c i j) -> p c j i", i=4, j=4),
-                    raw[a][:, :, c0 : c0 + P].rearrange("p j (c i) -> p c j i", i=4),
+                    raw[a][:].rearrange("p j (c i) -> p c j i", i=4),
                 )
-            codes = sb("w1_codes%d" % m, [P, 2 * P], U32)
-            plane = sb("w1_plane%d" % m, [P, 2 * P], U8)
+            codes = sb("w1_codes%d" % m, [P, 2 * width], U32)
+            plane = sb("w1_plane%d" % m, [P, 2 * width], U8)
             nc.vector.quantize_mx(
                 out=codes[:].bitcast(FP8X4), scales=plane[:], in_=grouped[:].rearrange("p a c -> p (a c)")
             )
-            stationary[m] = [(codes[:, P * a : P * (a + 1)], plane[:, P * a : P * (a + 1)]) for a in range(2)]
+            for e in range(width // P):
+                spans = [slice(width * a + P * e, width * a + P * (e + 1)) for a in range(2)]
+                stationary[m + e] = [(codes[:, span], plane[:, span]) for span in spans]
 
         def quantize_dealt(u):
             grouped = at(GROUPED_DEALT + 4 * KIB * u, "grouped_dealt%d" % u, [P, 2, 1024], BF16)
@@ -165,8 +166,14 @@ def tile_list_replay_slot_priority_kernel(
                 spans = [slice(P * (2 * a + e), P * (2 * a + e + 1)) for a in range(2)]
                 stationary[4 + 2 * u + e] = [(codes[:, span], plane[:, span]) for span in spans]
 
-        quantize_natural(0)
+        quantize_natural(0, raw_first, GROUPED_NATURAL + 4 * KIB)
         nc.vector.tensor_copy(v0[:], words[0][:].indirect(pick[:]))
+        weights = []
+        for m in range(4):
+            width = HALF if m == 0 else S
+            scaled = at(WEIGHTS + 4 * KIB * m, "weights%d" % m, [P, width], F32)
+            nc.vector.tensor_scalar_mul(scaled[:], wgs_rows[:, 0:width], gain_rows[:, m : m + 1])
+            weights.append(scaled)
         nc.vector.tensor_copy(v_plane[:], tab_plane[:].indirect(pick[:]))
         for s in range(2):
             nc.vector.tensor_copy(v1[s][:], words[1][:].indirect(pick[:, 32 * s : 32 * (s + 1)]))
@@ -199,51 +206,41 @@ def tile_list_replay_slot_priority_kernel(
                 )
             nc.scalar.activation(h[:, cols], acc[:, 0:width], ACT.Tanh, scale=-1.0)
 
-        def h_tile(m):
-            return at(H_RING + 4 * KIB * (m % H_SLOTS), "h%d" % m, [P, S], F32)
+        def h_tile(slot, name):
+            return at(H_RING + 4 * KIB * slot, name, [P, S], F32)
 
-        def weights_of(m, cols):
-            scaled = sb("weights%d" % m, [P, S], F32, tag="weights", bufs=2)
-            nc.gpsimd.tensor_scalar(scaled[:, cols], wgs_rows[:, cols], gain_rows[:, m : m + 1], 0.0, ALU.mult, ALU.add)
-            return scaled
-
-        def weighted(m):
-            h = h_tile(m)
-            if m < 4:
-                factor = weights_of(m, slice(0, S))[:]
-            elif m < 7:
-                factor = wgs_dealt[:, m - 4, :]
-            else:
-                factor = wgs_last[:]
+        def first_stage(m):
+            h = h_tile((0, 1, 2, 3, 4, 1, 2, 3)[m], "h%d" % m)
             for s in range(2):
-                first_stage_part(m, h, HALF * s, HALF, s + (6 if m == 7 else 0))
-            if m >= 4:
+                first_stage_part(m, h, HALF * s, HALF, (0, 0, 0, 2, 2, 4, 2, 4)[m] + s)
+            if m in (5, 6):
                 nc.scalar.activation(h[:], h[:], ACT.Copy, scale=gain_dealt[:, m - 4 : m - 3])
-            nc.gpsimd.tensor_tensor(h[:], h[:], factor, ALU.mult)
             return h
 
-        def page_of(m):
-            return pages[m % PAGES]
+        def weighted(m, h):
+            product = h_tile((4, 1, 2)[m - 5], "product%d" % m)
+            nc.gpsimd.tensor_tensor(product[:], h[:], wgs_dealt[:, m - 4, :], ALU.mult)
+            return product
 
-        def scatter(m, h, c0=0, width=S):
-            nc.vector.tensor_copy(
-                page_of(m)[:].indirect(place[:, c0 // 16 : (c0 + width) // 16]), h[:, c0 : c0 + width]
+        def page_of(m):
+            return pages[5 % PAGES] if m == 7 else pages[m % PAGES]
+
+        def scatter(m, h):
+            nc.vector.tensor_copy(page_of(m)[:].indirect(place[:]), h[:])
+
+        def scatter_weighted(m, h, factor, c0=0, width=S):
+            nc.vector.tensor_tensor(
+                page_of(m)[:].indirect(place[:, c0 // 16 : (c0 + width) // 16]), h[:, c0 : c0 + width], factor, ALU.mult
             )
 
-        h_first = h_tile(0)
-        weights_first = weights_of(0, slice(QUARTER, S))
-        for c0, width, b in ((0, QUARTER, 0), (QUARTER, QUARTER, 6), (HALF, HALF, 1)):
-            cols = slice(c0, c0 + width)
-            first_stage_part(0, h_first, c0, width, b)
-            if c0 == 0:
-                nc.vector.scalar_tensor_tensor(
-                    h_first[:, cols], h_first[:, cols], gain_rows[:, 0:1], wgs_rows[:, cols], ALU.mult, ALU.mult
-                )
-            else:
-                nc.gpsimd.tensor_tensor(h_first[:, cols], h_first[:, cols], weights_first[:, cols], ALU.mult)
-            scatter(0, h_first, c0, width)
-            if c0 == 0:
-                quantize_natural(1)
+        h_first = h_tile(0, "h0")
+        first_stage_part(0, h_first, 0, HALF, 0)
+        scatter_weighted(0, h_first, weights[0][:], 0, HALF)
+        first_stage_part(0, h_first, HALF, HALF, 1)
+        quantize_natural(1, raw_second, GROUPED_NATURAL)
+        weights_rest = at(GROUPED_NATURAL, "weights_rest", [P, HALF], F32)
+        nc.vector.tensor_scalar_mul(weights_rest[:], wgs_rows[:, HALF:S], gain_rows[:, 0:1])
+        scatter_weighted(0, h_first, weights_rest[:], HALF, HALF)
 
         turned = [at(RAW_NATURAL + 4 * KIB * ((c + 1) % CHUNKS), "turned%d" % c, [P, 4, 2, 256], BF16) for c in range(CHUNKS)]
 
@@ -269,26 +266,31 @@ def tile_list_replay_slot_priority_kernel(
                         ACT.Abs,
                     )
 
-        h_next = weighted(1)
-        quantize_natural(2)
-        quantize_natural(3)
-        scatter(1, h_next)
-        h_next = weighted(2)
+        h_next = first_stage(1)
+        quantize_natural(3, raw_third, GROUPED_NATURAL + 4 * KIB)
+        scatter_weighted(1, h_next, weights[1][:])
+        h_next = first_stage(2)
         quantize_dealt(0)
         difference_turned(0)
-        scatter(2, h_next)
-        h_next = weighted(3)
+        scatter_weighted(2, h_next, weights[2][:])
+        h_next = first_stage(3)
         quantize_dealt(1)
         difference_turned(1)
-        scatter(3, h_next)
-        h_dealt = [weighted(4), weighted(5)]
+        scatter_weighted(3, h_next, weights[3][:])
+        h_next = first_stage(4)
+        h_after = first_stage(5)
+        h_dealt = [h_tile(0, "product4")]
         difference_turned(2)
+        nc.vector.scalar_tensor_tensor(
+            h_dealt[0][:], h_next[:], gain_dealt[:, 0:1], wgs_dealt[:, 0, :], ALU.mult, ALU.mult
+        )
+        h_dealt.append(weighted(5, h_after))
         scatter(4, h_dealt[0])
-        h_dealt.append(weighted(6))
+        h_dealt.extend([weighted(m, first_stage(m)) for m in (6, 7)])
         difference_turned(3)
         scatter(5, h_dealt[1])
 
-        low = at(GROUPED_NATURAL, "low", [P, 2, T2], F32)
+        low = at(WGS_DEALT, "low", [P, 2, T2], F32)
 
         def sum_low(e):
             for half in range(2):
@@ -312,11 +314,12 @@ def tile_list_replay_slot_priority_kernel(
                 )
         w2_codes = at(RAW_NATURAL, "w2_codes", [P, 2, 2 * N], U8)
         nc.sync.dma_start(w2_codes[:].bitcast(I32), w2_words.rearrange("a p c -> p a c").bitcast(I32))
+        h_last = at(H_LAST, "h_last", [P, S], F32)
+        nc.scalar.activation(h_last[:], h_dealt[3][:], ACT.Copy, scale=gain_dealt[:, 3:4])
         scatter(6, h_dealt[2])
         sum_low(1)
-        h_last = weighted(7)
-        first_codes = sb("first_codes", [P, T2], U32)
-        first_plane = sb("first_plane", [P, T2], U8)
+        first_codes = at(WEIGHTS, "first_codes", [P, T2], U32)
+        first_plane = at(WEIGHTS + 8 * KIB, "first_plane", [P, T2], U8)
         for g in range(2):
             cols = slice(1024 * g, 1024 * (g + 1))
             nc.vector.quantize_mx(out=first_codes[:, cols].bitcast(FP8X4), scales=first_plane[:, cols], in_=z_first[g][:])

@@ -61,15 +61,12 @@ def tile_list_replay_slot_priority_kernel(
         tab_plane = sb("tab_plane", [P, T], U8)
         nc.vector.memset(tab_plane[:, 0 : T // 2].bitcast(I32), 0)
         nc.gpsimd.memset(tab_plane[:, T // 2 : T].bitcast(I32), 0)
-        pick = sb("pick", [P, S // 16], U16)
-        place = sb("place", [P, S // 16], U16)
-        nc.sync.dma_start(pick[:], offs)
-        nc.sync.dma_start(place[:], offs2)
-        gain_flat = sb("gain_flat", [P, P], F32)
-        nc.gpsimd.memset(gain_flat[:], 0.0)
-        gain_dealt = sb("gain_dealt", [P, 4], F32)
-        nc.sync.dma_start(gain_dealt[:], gain[512:1024].rearrange("(p i) -> p i", i=4))
-        nc.sync.dma_start(gain_flat[0:4, :], gain[0:512].rearrange("(m p) -> m p", p=P))
+        words = [at(offset, "words%d" % a, [P, T], U32) for a, offset in enumerate((WORDS0, WORDS1))]
+
+        def load_words(a, c0, c1):
+            nc.sync.dma_start(
+                words[a][:, c0:c1].bitcast(I32), tab_words[a].rearrange("p t i -> p (t i)").bitcast(I32)[:, c0:c1]
+            )
 
         def load_w1(offset, name, a, c0, width, parts=1):
             raw = at(offset, name, [P, 4, width], F32)
@@ -79,16 +76,19 @@ def tile_list_replay_slot_priority_kernel(
                 nc.sync.dma_start(raw[:, js, :], rows[:, js, :])
             return raw
 
+        load_words(0, 0, T // 4)
+        pick = sb("pick", [P, S // 16], U16)
+        place = sb("place", [P, S // 16], U16)
+        nc.sync.dma_start(pick[:], offs)
+        nc.sync.dma_start(place[:], offs2)
+        gain_flat = sb("gain_flat", [P, P], F32)
+        nc.gpsimd.memset(gain_flat[:], 0.0)
+        gain_dealt = sb("gain_dealt", [P, 4], F32)
+        nc.sync.dma_start(gain_dealt[:], gain[512:1024].rearrange("(p i) -> p i", i=4))
+        nc.sync.dma_start(gain_flat[0:4, :], gain[0:512].rearrange("(m p) -> m p", p=P))
+        for quarter in range(1, 4):
+            load_words(0, quarter * T // 4, (quarter + 1) * T // 4)
         raw_first = [load_w1(RAW_NATURAL + 2 * KIB * a, "raw_first%d" % a, a, 0, 128, 2) for a in range(2)]
-        words = [at(offset, "words%d" % a, [P, T], U32) for a, offset in enumerate((WORDS0, WORDS1))]
-
-        def load_words(a, cols):
-            nc.sync.dma_start(
-                words[a][:, cols].bitcast(I32), tab_words[a].rearrange("p t i -> p (t i)").bitcast(I32)[:, cols]
-            )
-
-        for piece in range(4):
-            load_words(0, slice(piece * T // 4, (piece + 1) * T // 4))
         wgs_rows = sb("wgs_rows", [P, S], F32)
         nc.sync.dma_start(wgs_rows[:], wgs)
         for q in range(4):
@@ -96,7 +96,7 @@ def tile_list_replay_slot_priority_kernel(
                 tab_plane[32 * q : 32 * q + 8, :].bitcast(I32),
                 tab_scales[:, 4 * q : 4 * q + 4, :].bitcast(I32),
             )
-        load_words(1, slice(0, T))
+        load_words(1, 0, T)
         raw_second = [load_w1(RAW_NATURAL + 4 * KIB + 4 * KIB * a, "raw_second%d" % a, a, 128, 256) for a in range(2)]
         raw_third = [load_w1(RAW_NATURAL + 12 * KIB + 2 * KIB * a, "raw_third%d" % a, a, 384, 128) for a in range(2)]
 
@@ -170,9 +170,8 @@ def tile_list_replay_slot_priority_kernel(
         nc.vector.tensor_copy(v0[:], words[0][:].indirect(pick[:]))
         weights = []
         for m in range(4):
-            width = HALF if m == 0 else S
-            scaled = at(WEIGHTS + 4 * KIB * m, "weights%d" % m, [P, width], F32)
-            nc.vector.tensor_scalar_mul(scaled[:], wgs_rows[:, 0:width], gain_rows[:, m : m + 1])
+            scaled = at(WEIGHTS + 4 * KIB * m, "weights%d" % m, [P, S], F32)
+            nc.vector.tensor_scalar_mul(scaled[:], wgs_rows[:], gain_rows[:, m : m + 1])
             weights.append(scaled)
         nc.vector.tensor_copy(v_plane[:], tab_plane[:].indirect(pick[:]))
         for s in range(2):
@@ -204,7 +203,7 @@ def tile_list_replay_slot_priority_kernel(
                     start=(a == 0),
                     stop=(a == 1),
                 )
-            nc.scalar.activation(h[:, cols], acc[:, 0:width], ACT.Tanh, scale=-1.0)
+            nc.scalar.activation(h, acc[:, 0:width], ACT.Tanh, scale=-1.0)
 
         def h_tile(slot, name):
             return at(H_RING + 4 * KIB * slot, name, [P, S], F32)
@@ -212,7 +211,7 @@ def tile_list_replay_slot_priority_kernel(
         def first_stage(m):
             h = h_tile((0, 1, 2, 3, 4, 1, 2, 3)[m], "h%d" % m)
             for s in range(2):
-                first_stage_part(m, h, HALF * s, HALF, (0, 0, 0, 2, 2, 4, 2, 4)[m] + s)
+                first_stage_part(m, h[:, HALF * s : HALF * (s + 1)], HALF * s, HALF, (0, 0, 0, 2, 2, 4, 2, 4)[m] + s)
             if m in (5, 6):
                 nc.scalar.activation(h[:], h[:], ACT.Copy, scale=gain_dealt[:, m - 4 : m - 3])
             return h
@@ -230,17 +229,18 @@ def tile_list_replay_slot_priority_kernel(
 
         def scatter_weighted(m, h, factor, c0=0, width=S):
             nc.vector.tensor_tensor(
-                page_of(m)[:].indirect(place[:, c0 // 16 : (c0 + width) // 16]), h[:, c0 : c0 + width], factor, ALU.mult
+                page_of(m)[:].indirect(place[:, c0 // 16 : (c0 + width) // 16]), h, factor, ALU.mult
             )
 
-        h_first = h_tile(0, "h0")
-        first_stage_part(0, h_first, 0, HALF, 0)
-        scatter_weighted(0, h_first, weights[0][:], 0, HALF)
-        first_stage_part(0, h_first, HALF, HALF, 1)
+        h_half = at(H_RING, "h0_first", [P, HALF], F32)
+        for c0, b in ((0, 0), (QUARTER, 6)):
+            cols = slice(c0, c0 + QUARTER)
+            first_stage_part(0, h_half[:, cols], c0, QUARTER, b)
+            scatter_weighted(0, h_half[:, cols], weights[0][:, cols], c0, QUARTER)
         quantize_natural(1, raw_second, GROUPED_NATURAL)
-        weights_rest = at(GROUPED_NATURAL, "weights_rest", [P, HALF], F32)
-        nc.vector.tensor_scalar_mul(weights_rest[:], wgs_rows[:, HALF:S], gain_rows[:, 0:1])
-        scatter_weighted(0, h_first, weights_rest[:], HALF, HALF)
+        h_half = at(RAW_NATURAL + 8 * KIB, "h0_second", [P, HALF], F32)
+        first_stage_part(0, h_half[:], HALF, HALF, 1)
+        scatter_weighted(0, h_half[:], weights[0][:, HALF:S], HALF, HALF)
 
         turned = [at(RAW_NATURAL + 4 * KIB * ((c + 1) % CHUNKS), "turned%d" % c, [P, 4, 2, 256], BF16) for c in range(CHUNKS)]
 
@@ -258,25 +258,23 @@ def tile_list_replay_slot_priority_kernel(
                             start=(step == 0 and b == 0),
                             stop=(step == 1 and b == 3),
                         )
-                src = acc[:].rearrange("p (b w u e) -> p u b w e", b=4, u=2, e=2)
-                for u in range(2):
-                    nc.scalar.activation(
-                        turned[c][:, :, u, 64 * m : 64 * (m + 1)].rearrange("p b (w e) -> p b w e", e=2),
-                        src[:, u],
-                        ACT.Abs,
-                    )
+                nc.scalar.activation(
+                    turned[c][:, :, :, 64 * m : 64 * (m + 1)].rearrange("p b u (w e) -> p u b w e", e=2),
+                    acc[:].rearrange("p (b w u e) -> p u b w e", b=4, u=2, e=2),
+                    ACT.Abs,
+                )
 
         h_next = first_stage(1)
         quantize_natural(3, raw_third, GROUPED_NATURAL + 4 * KIB)
-        scatter_weighted(1, h_next, weights[1][:])
+        scatter_weighted(1, h_next[:], weights[1][:])
         h_next = first_stage(2)
         quantize_dealt(0)
         difference_turned(0)
-        scatter_weighted(2, h_next, weights[2][:])
+        scatter_weighted(2, h_next[:], weights[2][:])
         h_next = first_stage(3)
         quantize_dealt(1)
         difference_turned(1)
-        scatter_weighted(3, h_next, weights[3][:])
+        scatter_weighted(3, h_next[:], weights[3][:])
         h_next = first_stage(4)
         h_after = first_stage(5)
         h_dealt = [h_tile(0, "product4")]
@@ -385,7 +383,10 @@ def tile_list_replay_slot_priority_kernel(
             staged = at(WORDS0 + 8 * t0, "staged%d" % k, [P, 2, width], F32)
             if wide:
                 for n in range(2):
-                    nc.scalar.copy(staged[:, n, :], accs[n])
+                    if k == 3 and n == 1:
+                        nc.vector.tensor_copy(staged[:, n, :], accs[n])
+                    else:
+                        nc.scalar.copy(staged[:, n, :], accs[n])
                     nc.sync.dma_start(out_rows[:, n, cols], staged[:, n, :])
             else:
                 if k == 0:

@@ -97,8 +97,9 @@ def tile_list_replay_slot_priority_kernel(
                 tab_scales[:, 4 * q : 4 * q + 4, :].bitcast(I32),
             )
         load_words(1, 0, T)
-        raw_second = [load_w1(RAW_NATURAL + 4 * KIB + 4 * KIB * a, "raw_second%d" % a, a, 128, 256) for a in range(2)]
-        raw_third = [load_w1(RAW_NATURAL + 12 * KIB + 2 * KIB * a, "raw_third%d" % a, a, 384, 128) for a in range(2)]
+        raw_natural = [raw_first]
+        for m, offset in ((1, RAW_NATURAL + 4 * KIB), (2, H_RING + 4 * KIB), (3, H_RING + 8 * KIB)):
+            raw_natural.append([load_w1(offset + 2 * KIB * a, "raw%d_%d" % (m, a), a, P * m, P) for a in range(2)])
 
         def load_old_rows(m):
             rows = at(OLD_ROWS + 8 * KIB * m, "old_rows%d" % m, [P, T2], F32)
@@ -107,12 +108,11 @@ def tile_list_replay_slot_priority_kernel(
 
         raw_dealt = [load_w1(RAW_DEALT + 8 * KIB * a, "raw_dealt%d" % a, a, 512, 512) for a in range(2)]
         old_rows = [load_old_rows(0)]
-        old_rows.append(load_old_rows(1))
+        old_rows.extend([load_old_rows(1), load_old_rows(2)])
         wgs_planes = wgs.rearrange("(m i) s -> m i s", i=4)
         wgs_dealt = at(WGS_DEALT, "wgs_dealt", [P, 4, S], F32)
         for q in (0, 2, 1, 3):
             nc.sync.dma_start(wgs_dealt[32 * q : 32 * (q + 1)], wgs_planes)
-        old_rows.append(load_old_rows(2))
         old_rows.append(load_old_rows(3))
 
         pages = [sb("page%d" % i, [P, T2], F32) for i in range(PAGES)]
@@ -133,40 +133,36 @@ def tile_list_replay_slot_priority_kernel(
         v_plane = sb("v_plane", [P, S], U8)
         stationary = {}
 
-        def quantize_natural(m, raw, offset):
-            width = raw[0].shape[2]
-            grouped = at(offset, "grouped%d" % m, [P, 2, width * 4], BF16)
+        def quantize_w1(name, grouped, first_tile):
+            words_wide = grouped.shape[2] // 4
+            codes = sb("w1_codes" + name, [P, 2 * words_wide], U32)
+            plane = sb("w1_plane" + name, [P, 2 * words_wide], U8)
+            nc.vector.quantize_mx(
+                out=codes[:].bitcast(FP8X4), scales=plane[:], in_=grouped[:].rearrange("p a c -> p (a c)")
+            )
+            for e in range(words_wide // P):
+                spans = [slice(words_wide * a + P * e, words_wide * a + P * (e + 1)) for a in range(2)]
+                stationary[first_tile + e] = [(codes[:, span], plane[:, span]) for span in spans]
+
+        def quantize_natural(m):
+            grouped = at(GROUPED_NATURAL + 2 * KIB * (m % 2), "grouped%d" % m, [P, 2, P * 4], BF16)
             for a in range(2):
                 nc.scalar.copy(
                     grouped[:, a, :].rearrange("p (c i j) -> p c j i", i=4, j=4),
-                    raw[a][:].rearrange("p j (c i) -> p c j i", i=4),
+                    raw_natural[m][a][:].rearrange("p j (c i) -> p c j i", i=4),
                 )
-            codes = sb("w1_codes%d" % m, [P, 2 * width], U32)
-            plane = sb("w1_plane%d" % m, [P, 2 * width], U8)
-            nc.vector.quantize_mx(
-                out=codes[:].bitcast(FP8X4), scales=plane[:], in_=grouped[:].rearrange("p a c -> p (a c)")
-            )
-            for e in range(width // P):
-                spans = [slice(width * a + P * e, width * a + P * (e + 1)) for a in range(2)]
-                stationary[m + e] = [(codes[:, span], plane[:, span]) for span in spans]
+            quantize_w1("%d" % m, grouped, m)
 
-        def quantize_dealt(u):
-            grouped = at(GROUPED_DEALT + 4 * KIB * u, "grouped_dealt%d" % u, [P, 2, 1024], BF16)
+        def quantize_dealt():
+            grouped = at(GROUPED_DEALT, "grouped_dealt", [P, 2, 2048], BF16)
             for a in range(2):
                 nc.scalar.copy(
-                    grouped[:, a, :].rearrange("p (e m j) -> p m j e", e=2, j=4),
-                    raw_dealt[a][:].rearrange("p j (m u e) -> p u m j e", u=2, e=2)[:, u],
+                    grouped[:, a, :].rearrange("p (i m j) -> p m j i", i=4, j=4),
+                    raw_dealt[a][:].rearrange("p j (m i) -> p m j i", i=4),
                 )
-            codes = sb("w1_codes_dealt%d" % u, [P, 512], U32)
-            plane = sb("w1_plane_dealt%d" % u, [P, 512], U8)
-            nc.vector.quantize_mx(
-                out=codes[:].bitcast(FP8X4), scales=plane[:], in_=grouped[:].rearrange("p a c -> p (a c)")
-            )
-            for e in range(2):
-                spans = [slice(P * (2 * a + e), P * (2 * a + e + 1)) for a in range(2)]
-                stationary[4 + 2 * u + e] = [(codes[:, span], plane[:, span]) for span in spans]
+            quantize_w1("_dealt", grouped, 4)
 
-        quantize_natural(0, raw_first, GROUPED_NATURAL + 4 * KIB)
+        quantize_natural(0)
         nc.vector.tensor_copy(v0[:], words[0][:].indirect(pick[:]))
         weights = []
         for m in range(4):
@@ -209,15 +205,18 @@ def tile_list_replay_slot_priority_kernel(
             return at(H_RING + 4 * KIB * slot, name, [P, S], F32)
 
         def first_stage(m):
-            h = h_tile((0, 1, 2, 3, 4, 1, 2, 3)[m], "h%d" % m)
+            if m in (3, 7):
+                h = at(RAW_DEALT + (8 * KIB if m == 3 else 0), "h%d" % m, [P, S], F32)
+            else:
+                h = h_tile({1: 1, 2: 2, 4: 4, 5: 3, 6: 1}[m], "h%d" % m)
             for s in range(2):
-                first_stage_part(m, h[:, HALF * s : HALF * (s + 1)], HALF * s, HALF, (0, 0, 0, 2, 2, 4, 2, 4)[m] + s)
+                first_stage_part(m, h[:, HALF * s : HALF * (s + 1)], HALF * s, HALF, 6 * (m % 2) + s)
             if m in (5, 6):
                 nc.scalar.activation(h[:], h[:], ACT.Copy, scale=gain_dealt[:, m - 4 : m - 3])
             return h
 
         def weighted(m, h):
-            product = h_tile((4, 1, 2)[m - 5], "product%d" % m)
+            product = h_tile((4, 3, 1)[m - 5], "product%d" % m)
             nc.gpsimd.tensor_tensor(product[:], h[:], wgs_dealt[:, m - 4, :], ALU.mult)
             return product
 
@@ -237,8 +236,8 @@ def tile_list_replay_slot_priority_kernel(
             cols = slice(c0, c0 + QUARTER)
             first_stage_part(0, h_half[:, cols], c0, QUARTER, b)
             scatter_weighted(0, h_half[:, cols], weights[0][:, cols], c0, QUARTER)
-        quantize_natural(1, raw_second, GROUPED_NATURAL)
-        h_half = at(RAW_NATURAL + 8 * KIB, "h0_second", [P, HALF], F32)
+        quantize_natural(1)
+        h_half = at(RAW_NATURAL + 6 * KIB, "h0_second", [P, HALF], F32)
         first_stage_part(0, h_half[:], HALF, HALF, 1)
         scatter_weighted(0, h_half[:], weights[0][:, HALF:S], HALF, HALF)
 
@@ -264,15 +263,15 @@ def tile_list_replay_slot_priority_kernel(
                     ACT.Abs,
                 )
 
+        quantize_natural(2)
         h_next = first_stage(1)
-        quantize_natural(3, raw_third, GROUPED_NATURAL + 4 * KIB)
         scatter_weighted(1, h_next[:], weights[1][:])
+        quantize_natural(3)
         h_next = first_stage(2)
-        quantize_dealt(0)
         difference_turned(0)
         scatter_weighted(2, h_next[:], weights[2][:])
+        quantize_dealt()
         h_next = first_stage(3)
-        quantize_dealt(1)
         difference_turned(1)
         scatter_weighted(3, h_next[:], weights[3][:])
         h_next = first_stage(4)

@@ -106,14 +106,17 @@ def tile_list_replay_slot_priority_kernel(
             nc.sync.dma_start(rows[:], old[P * m : P * (m + 1), :])
             return rows
 
-        raw_dealt = [load_w1(RAW_DEALT + 8 * KIB * a, "raw_dealt%d" % a, a, 512, 512) for a in range(2)]
+        raw_dealt = [load_w1(RAW_DEALT, "raw_dealt0", 0, 512, 512)]
         old_rows = [load_old_rows(0)]
-        old_rows.extend([load_old_rows(1), load_old_rows(2)])
-        wgs_planes = wgs.rearrange("(m i) s -> m i s", i=4)
-        wgs_dealt = at(WGS_DEALT, "wgs_dealt", [P, 4, S], F32)
-        for q in (0, 2, 1, 3):
-            nc.sync.dma_start(wgs_dealt[32 * q : 32 * (q + 1)], wgs_planes)
-        old_rows.append(load_old_rows(3))
+        raw_dealt.append(load_w1(RAW_DEALT + 8 * KIB, "raw_dealt1", 1, 512, 512))
+        wgs_dealt = []
+        for i in range(4):
+            if i < 3:
+                old_rows.append(load_old_rows(i + 1))
+            dealt = at(WGS_DEALT + 4 * KIB * i, "wgs_dealt%d" % i, [P, S], F32)
+            for q in (0, 2, 1, 3):
+                nc.sync.dma_start(dealt[32 * q : 32 * (q + 1), :], wgs[i:P:4, :])
+            wgs_dealt.append(dealt)
 
         pages = [sb("page%d" % i, [P, T2], F32) for i in range(PAGES)]
         for page in pages[:2]:
@@ -179,8 +182,9 @@ def tile_list_replay_slot_priority_kernel(
                 w2_plane[32 * q : 32 * q + 4].bitcast(I32),
                 w2_scales[:, 4 * q : 4 * q + 4, :].rearrange("a r c -> r a c").bitcast(I32),
             )
-        old_low = at(WORDS0, "old_low", [P, 2, T2], F32)
-        nc.sync.dma_start(old_low[:], old_dealt[0])
+        old_low = [at(WORDS0 + 8 * KIB * e, "old_low%d" % e, [P, T2], F32) for e in range(2)]
+        for e in range(2):
+            nc.sync.dma_start(old_low[e][:], old_dealt[0][:, e, :])
         old_high = at(WORDS1, "old_high", [P, 2, T2], F32)
         nc.sync.dma_start(old_high[:], old_dealt[1])
 
@@ -210,14 +214,14 @@ def tile_list_replay_slot_priority_kernel(
             else:
                 h = h_tile({1: 1, 2: 2, 4: 4, 5: 3, 6: 1}[m], "h%d" % m)
             for s in range(2):
-                first_stage_part(m, h[:, HALF * s : HALF * (s + 1)], HALF * s, HALF, 6 * (m % 2) + s)
+                first_stage_part(m, h[:, HALF * s : HALF * (s + 1)], HALF * s, HALF, (0, 6, 0, 2, 6, 0, 2, 4)[m] + s)
             if m in (5, 6):
                 nc.scalar.activation(h[:], h[:], ACT.Copy, scale=gain_dealt[:, m - 4 : m - 3])
             return h
 
         def weighted(m, h):
             product = h_tile((4, 3, 1)[m - 5], "product%d" % m)
-            nc.gpsimd.tensor_tensor(product[:], h[:], wgs_dealt[:, m - 4, :], ALU.mult)
+            nc.gpsimd.tensor_tensor(product[:], h[:], wgs_dealt[m - 4][:], ALU.mult)
             return product
 
         def page_of(m):
@@ -245,7 +249,7 @@ def tile_list_replay_slot_priority_kernel(
 
         def difference_turned(m):
             for c in range(CHUNKS):
-                acc = bank(2 + c, "fwd%d_%d" % (m, c))
+                acc = bank((2 + 4 * m + c) % 8, "fwd%d_%d" % (m, c))
                 for step, source in enumerate((old_rows[m], pages[m % PAGES])):
                     for b in range(4):
                         t0 = BANK * c + P * b
@@ -279,7 +283,7 @@ def tile_list_replay_slot_priority_kernel(
         h_dealt = [h_tile(0, "product4")]
         difference_turned(2)
         nc.vector.scalar_tensor_tensor(
-            h_dealt[0][:], h_next[:], gain_dealt[:, 0:1], wgs_dealt[:, 0, :], ALU.mult, ALU.mult
+            h_dealt[0][:], h_next[:], gain_dealt[:, 0:1], wgs_dealt[0][:], ALU.mult, ALU.mult
         )
         h_dealt.append(weighted(5, h_after))
         scatter(4, h_dealt[0])
@@ -292,13 +296,13 @@ def tile_list_replay_slot_priority_kernel(
         def sum_low(e):
             for half in range(2):
                 cols = slice(1024 * half, 1024 * (half + 1))
-                nc.gpsimd.tensor_tensor(low[:, e, cols], old_low[:, e, cols], pages[(4 + e) % PAGES][:, cols], ALU.add)
+                nc.gpsimd.tensor_tensor(low[:, e, cols], old_low[e][:, cols], pages[(4 + e) % PAGES][:, cols], ALU.add)
 
         sum_low(0)
         z_first = [at(RAW_DEALT + 8 * KIB * g, "z_first%d" % g, [P, 4096], BF16) for g in range(2)]
         for c in range(CHUNKS):
             for half in range(2):
-                acc = bank((6, 2, 4, 6)[c] + half, "back%d_%d" % (c, half))
+                acc = bank((2 + 2 * c + half) % 8, "back%d_%d" % (c, half))
                 for b in range(2):
                     for u in range(2):
                         col = P * (2 * b + u)

@@ -90,7 +90,7 @@ def tile_list_replay_slot_priority_kernel(
             load_words(0, quarter * T // 4, (quarter + 1) * T // 4)
         raw_first = [load_w1(RAW_NATURAL + 2 * KIB * a, "raw_first%d" % a, a, 0, 128, 2) for a in range(2)]
         wgs_rows = sb("wgs_rows", [P, S], F32)
-        nc.sync.dma_start(wgs_rows[:], wgs)
+        nc.sync.dma_start(wgs_rows[:, 0:HALF], wgs[:, 0:HALF])
         for q in range(4):
             nc.sync.dma_start(
                 tab_plane[32 * q : 32 * q + 8, :].bitcast(I32),
@@ -100,6 +100,8 @@ def tile_list_replay_slot_priority_kernel(
         raw_natural = [raw_first]
         for m, offset in ((1, RAW_NATURAL + 4 * KIB), (2, H_RING + 4 * KIB), (3, H_RING + 8 * KIB)):
             raw_natural.append([load_w1(offset + 2 * KIB * a, "raw%d_%d" % (m, a), a, P * m, P) for a in range(2)])
+            if m == 1:
+                nc.sync.dma_start(wgs_rows[:, HALF:S], wgs[:, HALF:S])
 
         def load_old_rows(m):
             rows = at(OLD_ROWS + 8 * KIB * m, "old_rows%d" % m, [P, T2], F32)
@@ -170,7 +172,7 @@ def tile_list_replay_slot_priority_kernel(
         weights = []
         for m in range(4):
             scaled = at(WEIGHTS + 4 * KIB * m, "weights%d" % m, [P, S], F32)
-            nc.vector.tensor_scalar_mul(scaled[:], wgs_rows[:], gain_rows[:, m : m + 1])
+            nc.vector.tensor_scalar_mul(scaled[:, 0:HALF], wgs_rows[:, 0:HALF], gain_rows[:, m : m + 1])
             weights.append(scaled)
         nc.vector.tensor_copy(v_plane[:], tab_plane[:].indirect(pick[:]))
         for s in range(2):
@@ -230,6 +232,9 @@ def tile_list_replay_slot_priority_kernel(
         def scatter(m, h):
             nc.vector.tensor_copy(page_of(m)[:].indirect(place[:]), h[:])
 
+        def finish_weights(m):
+            nc.scalar.activation(weights[m][:, HALF:S], wgs_rows[:, HALF:S], ACT.Copy, scale=gain_rows[:, m : m + 1])
+
         def scatter_weighted(m, h, factor, c0=0, width=S):
             nc.vector.tensor_tensor(
                 page_of(m)[:].indirect(place[:, c0 // 16 : (c0 + width) // 16]), h, factor, ALU.mult
@@ -243,6 +248,7 @@ def tile_list_replay_slot_priority_kernel(
         quantize_natural(1)
         h_half = at(RAW_NATURAL + 6 * KIB, "h0_second", [P, HALF], F32)
         first_stage_part(0, h_half[:], HALF, HALF, 1)
+        finish_weights(0)
         scatter_weighted(0, h_half[:], weights[0][:, HALF:S], HALF, HALF)
 
         turned = [at(RAW_NATURAL + 4 * KIB * ((c + 1) % CHUNKS), "turned%d" % c, [P, 4, 2, 256], BF16) for c in range(CHUNKS)]
@@ -269,14 +275,17 @@ def tile_list_replay_slot_priority_kernel(
 
         quantize_natural(2)
         h_next = first_stage(1)
+        finish_weights(1)
         scatter_weighted(1, h_next[:], weights[1][:])
         quantize_natural(3)
         h_next = first_stage(2)
         difference_turned(0)
+        finish_weights(2)
         scatter_weighted(2, h_next[:], weights[2][:])
         quantize_dealt()
         h_next = first_stage(3)
         difference_turned(1)
+        finish_weights(3)
         scatter_weighted(3, h_next[:], weights[3][:])
         h_next = first_stage(4)
         h_after = first_stage(5)

@@ -24,7 +24,7 @@ QUARTER = S // 4
 CHUNKS = T2 // BANK
 PAGES = 3
 H_SLOTS = 5
-PIECES = [(0, 256), (256, 512), (768, 512), (1280, 512), (1792, 256)]
+PIECES = [(0, 256), (256, 512), (768, 512), (1280, 256), (1536, 256), (1792, 256)]
 
 WORDS0 = 0
 WORDS1 = 16 * KIB
@@ -346,13 +346,17 @@ def tile_list_replay_slot_priority_kernel(
                 stop=stop,
             )
 
-        high, pair_words, sums = [], [], []
+        pair_words, sums = [], []
         next_bank = 0
+        sixth = []
+        for k in range(0, len(PIECES), 2):
+            t0, width = PIECES[k][0], PIECES[k][1] + PIECES[k + 1][1]
+            cols = slice(t0, t0 + width)
+            part = at(RAW_DEALT + 4 * t0, "sixth%d" % k, [P, width], F32)
+            nc.gpsimd.tensor_tensor(part[:], old_high[:, 0, cols], pages[6 % PAGES][:, cols], ALU.add)
+            sixth.extend([part[:, 0 : PIECES[k][1]], part[:, PIECES[k][1] : width]])
         for k, (t0, width) in enumerate(PIECES):
             cols = slice(t0, t0 + width)
-            piece = at(RAW_DEALT + 8 * t0, "high%d" % k, [P, 2, width], F32)
-            nc.gpsimd.tensor_tensor(piece[:, 0, :], old_high[:, 0, cols], pages[6 % PAGES][:, cols], ALU.add)
-            high.append(piece)
             both = at(PAIR_WORDS + 8 * t0, "pair_words%d" % k, [P, 2, 2 * width], BF16)
             nc.scalar.activation(
                 both[:, 0, :].rearrange("p (t e) -> p t e", e=2), low[:, :, cols].rearrange("p e t -> p t e"), ACT.Abs
@@ -365,44 +369,80 @@ def tile_list_replay_slot_priority_kernel(
             for n in range(2):
                 second_pass(accs[n], 0, n, first_codes[:, cols], first_plane[:, cols], wide or n == 0, False)
             sums.append((banks, accs))
+        for k, (t0, width) in enumerate(PIECES):
+            nc.scalar.activation(pair_words[k][:, 1, 0 : 2 * width : 2], sixth[k], ACT.Abs)
 
         out_rows = out.rearrange("(n p) t -> p n t", p=P)
-        for k, (t0, width) in enumerate(PIECES):
+        seventh, woven, staged = {}, {}, {}
+
+        def add_last(k):
+            t0, width = PIECES[k]
             cols = slice(t0, t0 + width)
-            wide = width == BANK
-            nc.vector.tensor_tensor(high[k][:, 1, :], old_high[:, 1, cols], page_of(7)[:, cols], ALU.add)
-            nc.scalar.activation(
-                pair_words[k][:, 1, :].rearrange("p (t e) -> p t e", e=2),
-                high[k][:].rearrange("p e t -> p t e"),
-                ACT.Abs,
-            )
-            z = at(OLD_ROWS + 8 * t0, "z_second%d" % k, [P, 4 * width], BF16)
+            seventh[k] = at(RAW_DEALT + 4 * t0, "seventh%d" % k, [P, width], F32)
+            nc.vector.tensor_tensor(seventh[k][:], old_high[:, 1, cols], page_of(7)[:, cols], ALU.add)
+
+        def abs_last(k):
+            nc.scalar.activation(pair_words[k][:, 1, 1 : 2 * PIECES[k][1] : 2], seventh[k][:], ACT.Abs)
+
+        def weave(k):
+            t0, width = PIECES[k]
+            woven[k] = at(OLD_ROWS + 8 * t0, "z_second%d" % k, [P, 4 * width], BF16)
             nc.vector.tensor_copy(
-                z[:].bitcast(I32).rearrange("p (t u) -> p t u", u=2),
+                woven[k][:].bitcast(I32).rearrange("p (t u) -> p t u", u=2),
                 pair_words[k][:].bitcast(I32).rearrange("p u t -> p t u"),
             )
+
+        def finish(k):
+            width = PIECES[k][1]
+            wide = width == BANK
             codes = sb("second_codes%d" % k, [P, width], U32)
             plane = sb("second_plane%d" % k, [P, width], U8)
-            nc.vector.quantize_mx(out=codes[:].bitcast(FP8X4), scales=plane[:], in_=z[:])
-            banks, accs = sums[k]
+            nc.vector.quantize_mx(out=codes[:].bitcast(FP8X4), scales=plane[:], in_=woven[k][:])
             for n in range(2):
-                second_pass(accs[n], 1, n, codes[:], plane[:], False, wide or n == 1)
+                second_pass(sums[k][1][n], 1, n, codes[:], plane[:], False, wide or n == 1)
 
-        for k, (t0, width) in enumerate(PIECES):
+        def store(k, n, copy):
+            t0, width = PIECES[k]
             cols = slice(t0, t0 + width)
-            wide = width == BANK
             banks, accs = sums[k]
-            staged = at(WORDS0 + 8 * t0, "staged%d" % k, [P, 2, width], F32)
-            if wide:
-                for n in range(2):
-                    if k == 3 and n == 1:
-                        nc.vector.tensor_copy(staged[:, n, :], accs[n])
-                    else:
-                        nc.scalar.copy(staged[:, n, :], accs[n])
-                    nc.sync.dma_start(out_rows[:, n, cols], staged[:, n, :])
+            if k not in staged:
+                staged[k] = at(WORDS0 + 8 * t0, "staged%d" % k, [P, 2, width], F32)
+            if width == BANK:
+                copy(staged[k][:, n, :], accs[n])
+                nc.sync.dma_start(out_rows[:, n, cols], staged[k][:, n, :])
             else:
-                if k == 0:
-                    nc.scalar.copy(staged[:].rearrange("p n t -> p (n t)"), banks[0][:])
-                else:
-                    nc.vector.tensor_copy(staged[:].rearrange("p n t -> p (n t)"), banks[0][:])
-                nc.sync.dma_start(out_rows[:, :, cols], staged[:])
+                copy(staged[k][:].rearrange("p n t -> p (n t)"), banks[0][:])
+                nc.sync.dma_start(out_rows[:, :, cols], staged[k][:])
+
+        add_last(0)
+        add_last(1)
+        add_last(2)
+        abs_last(0)
+        abs_last(1)
+        abs_last(2)
+        weave(0)
+        add_last(3)
+        add_last(4)
+        abs_last(3)
+        abs_last(4)
+        finish(0)
+        weave(1)
+        add_last(5)
+        store(0, 0, nc.scalar.copy)
+        abs_last(5)
+        finish(1)
+        weave(2)
+        weave(3)
+        store(1, 0, nc.scalar.copy)
+        store(1, 1, nc.scalar.copy)
+        finish(2)
+        finish(3)
+        weave(4)
+        weave(5)
+        finish(4)
+        finish(5)
+        store(2, 0, nc.scalar.copy)
+        store(2, 1, nc.scalar.copy)
+        store(3, 0, nc.vector.tensor_copy)
+        store(4, 0, nc.scalar.copy)
+        store(5, 0, nc.vector.tensor_copy)

@@ -58,9 +58,9 @@ def tile_list_replay_slot_priority_kernel(
         def bank(b, name):
             return psum.tile([P, BANK], F32, name=name, tag="bank%d" % b)
 
-        tab_plane = sb("tab_plane", [P, T], U8)
-        nc.vector.memset(tab_plane[:, 0 : T // 2].bitcast(I32), 0)
-        nc.gpsimd.memset(tab_plane[:, T // 2 : T].bitcast(I32), 0)
+        tab_rows = at(GROUPED_DEALT, "tab_rows", [P, 2, T], U8)
+        nc.vector.memset(tab_rows[:, 0, :].bitcast(I32), 0)
+        nc.gpsimd.memset(tab_rows[:, 1, :].bitcast(I32), 0)
         words = [at(offset, "words%d" % a, [P, T], U32) for a, offset in enumerate((WORDS0, WORDS1))]
 
         def load_words(a, c0, c1):
@@ -77,31 +77,26 @@ def tile_list_replay_slot_priority_kernel(
             return raw
 
         load_words(0, 0, T // 4)
+        nc.sync.dma_start(tab_rows[0:P:8].bitcast(I32), tab_scales.rearrange("a q t -> q a t").bitcast(I32))
         pick = sb("pick", [P, S // 16], U16)
         place = sb("place", [P, S // 16], U16)
         nc.sync.dma_start(pick[:], offs)
-        nc.sync.dma_start(place[:], offs2)
         gain_flat = sb("gain_flat", [P, P], F32)
         nc.gpsimd.memset(gain_flat[:], 0.0)
-        gain_dealt = sb("gain_dealt", [P, 4], F32)
-        nc.sync.dma_start(gain_dealt[:], gain[512:1024].rearrange("(p i) -> p i", i=4))
         nc.sync.dma_start(gain_flat[0:4, :], gain[0:512].rearrange("(m p) -> m p", p=P))
-        for quarter in range(1, 4):
-            load_words(0, quarter * T // 4, (quarter + 1) * T // 4)
-        raw_first = [load_w1(RAW_NATURAL + 2 * KIB * a, "raw_first%d" % a, a, 0, 128, 2) for a in range(2)]
+        load_words(0, T // 4, T)
+        raw_first = [load_w1(RAW_NATURAL + 2 * KIB * a, "raw_first%d" % a, a, 0, 128) for a in range(2)]
         wgs_rows = sb("wgs_rows", [P, S], F32)
         nc.sync.dma_start(wgs_rows[:, 0:HALF], wgs[:, 0:HALF])
-        for q in range(4):
-            nc.sync.dma_start(
-                tab_plane[32 * q : 32 * q + 8, :].bitcast(I32),
-                tab_scales[:, 4 * q : 4 * q + 4, :].bitcast(I32),
-            )
         load_words(1, 0, T)
+        nc.sync.dma_start(place[:], offs2)
         raw_natural = [raw_first]
         for m, offset in ((1, RAW_NATURAL + 4 * KIB), (2, H_RING + 4 * KIB), (3, H_RING + 8 * KIB)):
             raw_natural.append([load_w1(offset + 2 * KIB * a, "raw%d_%d" % (m, a), a, P * m, P) for a in range(2)])
             if m == 1:
                 nc.sync.dma_start(wgs_rows[:, HALF:S], wgs[:, HALF:S])
+        gain_dealt = sb("gain_dealt", [P, 4], F32)
+        nc.sync.dma_start(gain_dealt[:], gain[512:1024].rearrange("(p i) -> p i", i=4))
 
         def load_old_rows(m):
             rows = at(OLD_ROWS + 8 * KIB * m, "old_rows%d" % m, [P, T2], F32)
@@ -121,21 +116,28 @@ def tile_list_replay_slot_priority_kernel(
             wgs_dealt.append(dealt)
 
         pages = [sb("page%d" % i, [P, T2], F32) for i in range(PAGES)]
-        for page in pages[:2]:
-            nc.vector.memset(page[:], 0.0)
         ident = sb("ident", [P, P], F32)
         make_identity(nc, ident[:])
-        nc.gpsimd.memset(pages[2][:], 0.0)
+        v_plane = sb("v_plane", [P, 2, S], U8)
+        nc.gpsimd.memset(v_plane[:].rearrange("p a s -> p (a s)").bitcast(I32), 0)
+        for page in pages:
+            nc.gpsimd.memset(page[:], 0.0)
         gain_rows = sb("gain_rows", [P, 4], F32)
         gain_bank = bank(7, "gain_bank")
         nc.tensor.transpose(gain_bank[:, 0:P], gain_flat[:], ident[:])
         nc.scalar.copy(gain_rows[:], gain_bank[:, 0:4])
         w2_plane = sb("w2_plane", [P, 2, N], U8)
-        nc.vector.memset(w2_plane[:].rearrange("p a c -> p (a c)").bitcast(I32), 0)
+        nc.gpsimd.memset(w2_plane[:].rearrange("p a c -> p (a c)").bitcast(I32), 0)
 
         v0 = sb("v0", [P, S], U32)
         v1 = [sb("v1_%d" % s, [P, HALF], U32) for s in range(2)]
-        v_plane = sb("v_plane", [P, S], U8)
+        picked_rows = sb("picked_rows", [P, 2, S], U8)
+        for a in range(2):
+            nc.vector.tensor_copy(picked_rows[:, a, :], tab_rows[:, a, :].indirect(pick[:]))
+        for q in range(4):
+            nc.scalar.dma_start(
+                v_plane[32 * q : 32 * q + 4].bitcast(I32), picked_rows[32 * q : 32 * (q + 1) : 8].bitcast(I32)
+            )
         stationary = {}
 
         def quantize_w1(name, grouped, first_tile):
@@ -174,7 +176,6 @@ def tile_list_replay_slot_priority_kernel(
             scaled = at(WEIGHTS + 4 * KIB * m, "weights%d" % m, [P, S], F32)
             nc.vector.tensor_scalar_mul(scaled[:, 0:HALF], wgs_rows[:, 0:HALF], gain_rows[:, m : m + 1])
             weights.append(scaled)
-        nc.vector.tensor_copy(v_plane[:], tab_plane[:].indirect(pick[:]))
         for s in range(2):
             nc.vector.tensor_copy(v1[s][:], words[1][:].indirect(pick[:, 32 * s : 32 * (s + 1)]))
 
@@ -201,7 +202,7 @@ def tile_list_replay_slot_priority_kernel(
                     lhsT=codes.bitcast(FP8X4),
                     lhsT_scale=plane,
                     rhs=moving.bitcast(FP8X4),
-                    rhs_scale=v_plane[4 * a : P, cols],
+                    rhs_scale=v_plane[:, a, cols],
                     start=(a == 0),
                     stop=(a == 1),
                 )

@@ -84,11 +84,12 @@ def tile_list_replay_slot_priority_kernel(
         gain_flat = sb("gain_flat", [P, P], F32)
         nc.gpsimd.memset(gain_flat[:], 0.0)
         nc.sync.dma_start(gain_flat[0:4, :], gain[0:512].rearrange("(m p) -> m p", p=P))
-        load_words(0, T // 4, T)
+        load_words(0, T // 4, T // 2)
+        load_words(0, T // 2, T)
         raw_first = [load_w1(RAW_NATURAL + 2 * KIB * a, "raw_first%d" % a, a, 0, 128) for a in range(2)]
         wgs_rows = sb("wgs_rows", [P, S], F32)
-        nc.sync.dma_start(wgs_rows[:, 0:HALF], wgs[:, 0:HALF])
         load_words(1, 0, T)
+        nc.sync.dma_start(wgs_rows[:, 0:HALF], wgs[:, 0:HALF])
         nc.sync.dma_start(place[:], offs2)
         raw_natural = [raw_first]
         for m, offset in ((1, RAW_NATURAL + 4 * KIB), (2, H_RING + 4 * KIB), (3, H_RING + 8 * KIB)):
@@ -172,9 +173,9 @@ def tile_list_replay_slot_priority_kernel(
         quantize_natural(0)
         nc.vector.tensor_copy(v0[:], words[0][:].indirect(pick[:]))
         weights = []
-        for m in range(4):
+        for m in range(2):
             scaled = at(WEIGHTS + 4 * KIB * m, "weights%d" % m, [P, S], F32)
-            nc.vector.tensor_scalar_mul(scaled[:, 0:HALF], wgs_rows[:, 0:HALF], gain_rows[:, m : m + 1])
+            nc.scalar.activation(scaled[:, 0:HALF], wgs_rows[:, 0:HALF], ACT.Copy, scale=gain_rows[:, m : m + 1])
             weights.append(scaled)
         for s in range(2):
             nc.vector.tensor_copy(v1[s][:], words[1][:].indirect(pick[:, 32 * s : 32 * (s + 1)]))
@@ -234,7 +235,10 @@ def tile_list_replay_slot_priority_kernel(
             nc.vector.tensor_copy(page_of(m)[:].indirect(place[:]), h[:])
 
         def finish_weights(m):
-            nc.scalar.activation(weights[m][:, HALF:S], wgs_rows[:, HALF:S], ACT.Copy, scale=gain_rows[:, m : m + 1])
+            if m >= 2:
+                weights.append(at(WEIGHTS + 4 * KIB * (m - 2), "weights%d" % m, [P, S], F32))
+            cols = slice(HALF if m < 2 else 0, S)
+            nc.scalar.activation(weights[m][:, cols], wgs_rows[:, cols], ACT.Copy, scale=gain_rows[:, m : m + 1])
 
         def scatter_weighted(m, h, factor, c0=0, width=S):
             nc.vector.tensor_tensor(

@@ -225,7 +225,10 @@ def tile_list_replay_slot_priority_kernel(
 
         def weighted(m, h):
             product = h_tile((4, 3, 1)[m - 5], "product%d" % m)
-            nc.gpsimd.tensor_tensor(product[:], h[:], wgs_dealt[m - 4][:], ALU.mult)
+            width = QUARTER if m == 7 else S
+            for c0 in range(0, S, width):
+                cols = slice(c0, c0 + width)
+                nc.gpsimd.tensor_tensor(product[:, cols], h[:, cols], wgs_dealt[m - 4][:, cols], ALU.mult)
             return product
 
         def page_of(m):
@@ -308,8 +311,9 @@ def tile_list_replay_slot_priority_kernel(
         low = at(WGS_DEALT, "low", [P, 2, T2], F32)
 
         def sum_low(e):
-            for half in range(2):
-                cols = slice(1024 * half, 1024 * (half + 1))
+            width = QUARTER if e == 0 else S
+            for t0 in range(0, T2, width):
+                cols = slice(t0, t0 + width)
                 nc.gpsimd.tensor_tensor(low[:, e, cols], old_low[e][:, cols], pages[(4 + e) % PAGES][:, cols], ALU.add)
 
         sum_low(0)

@@ -23,6 +23,7 @@ HALF = S // 2
 QUARTER = S // 4
 CHUNKS = T2 // BANK
 PAGES = 3
+ZEROED_FIRST = 768
 H_SLOTS = 5
 PIECES = [(0, 256), (256, 512), (768, 512), (1280, 256), (1536, 256), (1792, 256)]
 
@@ -38,6 +39,7 @@ WEIGHTS = 117 * KIB
 H_RING = 133 * KIB
 GROUPED_DEALT = H_RING + 4 * KIB * H_SLOTS
 GROUPED_NATURAL = GROUPED_DEALT + 8 * KIB
+LAST_PAGE = GROUPED_NATURAL + 4 * KIB
 
 
 def tile_list_replay_slot_priority_kernel(
@@ -58,9 +60,10 @@ def tile_list_replay_slot_priority_kernel(
         def bank(b, name):
             return psum.tile([P, BANK], F32, name=name, tag="bank%d" % b)
 
-        tab_rows = at(GROUPED_DEALT, "tab_rows", [P, 2, T], U8)
-        nc.vector.memset(tab_rows[:, 0, :].bitcast(I32), 0)
-        nc.gpsimd.memset(tab_rows[:, 1, :].bitcast(I32), 0)
+        tab_rows = at(LAST_PAGE, "tab_rows", [P, 2, T], U8)
+        row_words = tab_rows[:].rearrange("p a t -> p (a t)").bitcast(I32)
+        nc.gpsimd.memset(row_words[:, 0:ZEROED_FIRST], 0)
+        nc.vector.memset(row_words[:, ZEROED_FIRST : T // 2], 0)
         words = [at(offset, "words%d" % a, [P, T], U32) for a, offset in enumerate((WORDS0, WORDS1))]
 
         def load_words(a, c0, c1):
@@ -116,19 +119,19 @@ def tile_list_replay_slot_priority_kernel(
                 nc.sync.dma_start(dealt[32 * q : 32 * (q + 1), :], wgs[i:P:4, :])
             wgs_dealt.append(dealt)
 
-        pages = [sb("page%d" % i, [P, T2], F32) for i in range(PAGES)]
+        pages = [sb("page%d" % i, [P, T2], F32) for i in range(PAGES - 1)]
         ident = sb("ident", [P, P], F32)
         make_identity(nc, ident[:])
         v_plane = sb("v_plane", [P, 2, S], U8)
-        nc.gpsimd.memset(v_plane[:].rearrange("p a s -> p (a s)").bitcast(I32), 0)
+        nc.vector.memset(v_plane[:].rearrange("p a s -> p (a s)").bitcast(I32), 0)
         for page in pages:
-            nc.gpsimd.memset(page[:], 0.0)
+            nc.vector.memset(page[:].bitcast(I32), 0)
         gain_rows = sb("gain_rows", [P, 4], F32)
         gain_bank = bank(7, "gain_bank")
         nc.tensor.transpose(gain_bank[:, 0:P], gain_flat[:], ident[:])
         nc.scalar.copy(gain_rows[:], gain_bank[:, 0:4])
         w2_plane = sb("w2_plane", [P, 2, N], U8)
-        nc.gpsimd.memset(w2_plane[:].rearrange("p a c -> p (a c)").bitcast(I32), 0)
+        nc.vector.memset(w2_plane[:].rearrange("p a c -> p (a c)").bitcast(I32), 0)
 
         v0 = sb("v0", [P, S], U32)
         v1 = [sb("v1_%d" % s, [P, HALF], U32) for s in range(2)]
@@ -172,6 +175,8 @@ def tile_list_replay_slot_priority_kernel(
 
         quantize_natural(0)
         nc.vector.tensor_copy(v0[:], words[0][:].indirect(pick[:]))
+        pages.append(at(LAST_PAGE, "page2", [P, T2], F32))
+        nc.vector.memset(pages[2][:].bitcast(I32), 0)
         weights = []
         for m in range(2):
             scaled = at(WEIGHTS + 4 * KIB * m, "weights%d" % m, [P, S], F32)

from contextlib import ExitStack

import concourse.mybir as mybir
from concourse.masks import make_identity

K, T, S, T2, H, N, P = 1024, 4096, 1024, 2048, 1024, 256, 128
FLOPS = 2 * K * H * S + 2 * H * N * T2

F32 = mybir.dt.float32
BF16 = mybir.dt.bfloat16
I32 = mybir.dt.int32
U32 = mybir.dt.uint32
U16 = mybir.dt.uint16
U8 = mybir.dt.uint8
FP8X4 = mybir.dt.float8_e4m3fn_x4
FP4X4 = mybir.dt.float4_e2m1fn_x4
ACT = mybir.ActivationFunctionType
ALU = mybir.AluOpType

KIB = 1024
BANK = 512
HALF = S // 2
QUARTER = S // 4
CHUNKS = T2 // BANK
PAGES = 3
ZEROED_FIRST = 768
H_SLOTS = 5
PIECES = [(0, 256), (256, 512), (768, 512), (1280, 256), (1536, 256), (1792, 256)]

WORDS0 = 0
WORDS1 = 16 * KIB
RAW_NATURAL = 32 * KIB
H_LAST = 33 * KIB
PAIR_WORDS = 37 * KIB
RAW_DEALT = 53 * KIB
WGS_DEALT = 69 * KIB
OLD_ROWS = 85 * KIB
WEIGHTS = 117 * KIB
H_RING = 133 * KIB
GROUPED_DEALT = H_RING + 4 * KIB * H_SLOTS
GROUPED_NATURAL = GROUPED_DEALT + 8 * KIB
LAST_PAGE = GROUPED_NATURAL + 4 * KIB


def tile_list_replay_slot_priority_kernel(
    tc, tab_words, tab_scales, offs, w1, gain, wgs, offs2, old, w2_words, w2_scales, out
):
    nc = tc.nc
    with ExitStack() as ctx:
        keep = ctx.enter_context(tc.tile_pool(name="keep", bufs=1))
        shared = ctx.enter_context(tc.tile_pool(name="shared", bufs=1))
        psum = ctx.enter_context(tc.psum_pool(name="psum", bufs=1))

        def sb(name, shape, dtype, tag=None, bufs=1):
            return keep.tile(shape, dtype, name=name, tag=tag or name, bufs=bufs, align_bytes=64)

        def at(offset, name, shape, dtype):
            return shared.tile(shape, dtype, name=name, offset=offset, align_bytes=64)

        def bank(b, name):
            return psum.tile([P, BANK], F32, name=name, tag="bank%d" % b)

        tab_rows = at(LAST_PAGE, "tab_rows", [P, 2, T], U8)
        row_words = tab_rows[:].rearrange("p a t -> p (a t)").bitcast(I32)
        nc.gpsimd.memset(row_words[:, 0:ZEROED_FIRST], 0)
        nc.vector.memset(row_words[:, ZEROED_FIRST : T // 2], 0)
        words = [at(offset, "words%d" % a, [P, T], U32) for a, offset in enumerate((WORDS0, WORDS1))]

        def load_words(a, c0, c1):
            nc.sync.dma_start(
                words[a][:, c0:c1].bitcast(I32), tab_words[a].rearrange("p t i -> p (t i)").bitcast(I32)[:, c0:c1]
            )

        def load_w1(offset, name, a, c0, width, parts=1):
            raw = at(offset, name, [P, 4, width], F32)
            rows = w1[512 * a : 512 * (a + 1), c0 : c0 + width].rearrange("(p j) c -> p j c", j=4)
            for part in range(parts):
                js = slice(4 * part // parts, 4 * (part + 1) // parts)
                nc.sync.dma_start(raw[:, js, :], rows[:, js, :])
            return raw

        load_words(0, 0, T // 4)
        nc.sync.dma_start(tab_rows[0:P:8].bitcast(I32), tab_scales.rearrange("a q t -> q a t").bitcast(I32))
        pick = sb("pick", [P, S // 16], U16)
        place = sb("place", [P, S // 16], U16)
        nc.sync.dma_start(pick[:], offs)
        gain_flat = sb("gain_flat", [P, P], F32)
        nc.gpsimd.memset(gain_flat[:], 0.0)
        nc.sync.dma_start(gain_flat[0:4, :], gain[0:512].rearrange("(m p) -> m p", p=P))
        load_words(0, T // 4, T // 2)
        load_words(0, T // 2, T)
        raw_first = [load_w1(RAW_NATURAL + 2 * KIB * a, "raw_first%d" % a, a, 0, 128) for a in range(2)]
        wgs_rows = sb("wgs_rows", [P, S], F32)
        load_words(1, 0, T)
        nc.sync.dma_start(wgs_rows[:, 0:HALF], wgs[:, 0:HALF])
        nc.sync.dma_start(place[:], offs2)
        raw_natural = [raw_first]
        for m, offset in ((1, RAW_NATURAL + 4 * KIB), (2, H_RING + 4 * KIB), (3, H_RING + 8 * KIB)):
            raw_natural.append([load_w1(offset + 2 * KIB * a, "raw%d_%d" % (m, a), a, P * m, P) for a in range(2)])
            if m == 1:
                nc.sync.dma_start(wgs_rows[:, HALF:S], wgs[:, HALF:S])
        gain_dealt = sb("gain_dealt", [P, 4], F32)
        nc.sync.dma_start(gain_dealt[:], gain[512:1024].rearrange("(p i) -> p i", i=4))

        def load_old_rows(m):
            rows = at(OLD_ROWS + 8 * KIB * m, "old_rows%d" % m, [P, T2], F32)
            nc.sync.dma_start(rows[:], old[P * m : P * (m + 1), :])
            return rows

        raw_dealt = [load_w1(RAW_DEALT, "raw_dealt0", 0, 512, 512)]
        old_rows = [load_old_rows(0)]
        raw_dealt.append(load_w1(RAW_DEALT + 8 * KIB, "raw_dealt1", 1, 512, 512))
        wgs_dealt = []
        for i in range(4):
            if i < 3:
                old_rows.append(load_old_rows(i + 1))
            dealt = at(WGS_DEALT + 4 * KIB * i, "wgs_dealt%d" % i, [P, S], F32)
            for q in (0, 2, 1, 3):
                nc.sync.dma_start(dealt[32 * q : 32 * (q + 1), :], wgs[i:P:4, :])
            wgs_dealt.append(dealt)

        pages = [sb("page%d" % i, [P, T2], F32) for i in range(PAGES - 1)]
        ident = sb("ident", [P, P], F32)
        make_identity(nc, ident[:])
        v_plane = sb("v_plane", [P, 2, S], U8)
        nc.vector.memset(v_plane[:].rearrange("p a s -> p (a s)").bitcast(I32), 0)
        for page in pages:
            nc.vector.memset(page[:].bitcast(I32), 0)
        gain_rows = sb("gain_rows", [P, 4], F32)
        gain_bank = bank(7, "gain_bank")
        nc.tensor.transpose(gain_bank[:, 0:P], gain_flat[:], ident[:])
        nc.scalar.copy(gain_rows[:], gain_bank[:, 0:4])
        w2_plane = sb("w2_plane", [P, 2, N], U8)
        nc.vector.memset(w2_plane[:].rearrange("p a c -> p (a c)").bitcast(I32), 0)

        v0 = sb("v0", [P, S], U32)
        v1 = [sb("v1_%d" % s, [P, HALF], U32) for s in range(2)]
        picked_rows = sb("picked_rows", [P, 2, S], U8)
        for a in range(2):
            nc.vector.tensor_copy(picked_rows[:, a, :], tab_rows[:, a, :].indirect(pick[:]))
        for q in range(4):
            nc.scalar.dma_start(
                v_plane[32 * q : 32 * q + 4].bitcast(I32), picked_rows[32 * q : 32 * (q + 1) : 8].bitcast(I32)
            )
        stationary = {}

        def quantize_w1(name, grouped, first_tile):
            words_wide = grouped.shape[2] // 4
            codes = sb("w1_codes" + name, [P, 2 * words_wide], U32)
            plane = sb("w1_plane" + name, [P, 2 * words_wide], U8)
            nc.vector.quantize_mx(
                out=codes[:].bitcast(FP8X4), scales=plane[:], in_=grouped[:].rearrange("p a c -> p (a c)")
            )
            for e in range(words_wide // P):
                spans = [slice(words_wide * a + P * e, words_wide * a + P * (e + 1)) for a in range(2)]
                stationary[first_tile + e] = [(codes[:, span], plane[:, span]) for span in spans]

        def quantize_natural(m):
            grouped = at(GROUPED_NATURAL + 2 * KIB * (m % 2), "grouped%d" % m, [P, 2, P * 4], BF16)
            for a in range(2):
                nc.scalar.copy(
                    grouped[:, a, :].rearrange("p (c i j) -> p c j i", i=4, j=4),
                    raw_natural[m][a][:].rearrange("p j (c i) -> p c j i", i=4),
                )
            quantize_w1("%d" % m, grouped, m)

        def quantize_dealt():
            grouped = at(GROUPED_DEALT, "grouped_dealt", [P, 2, 2048], BF16)
            for a in range(2):
                nc.scalar.copy(
                    grouped[:, a, :].rearrange("p (i m j) -> p m j i", i=4, j=4),
                    raw_dealt[a][:].rearrange("p j (m i) -> p m j i", i=4),
                )
            quantize_w1("_dealt", grouped, 4)

        quantize_natural(0)
        nc.vector.tensor_copy(v0[:], words[0][:].indirect(pick[:]))
        pages.append(at(LAST_PAGE, "page2", [P, T2], F32))
        nc.vector.memset(pages[2][:].bitcast(I32), 0)
        weights = []
        for m in range(2):
            scaled = at(WEIGHTS + 4 * KIB * m, "weights%d" % m, [P, S], F32)
            nc.scalar.activation(scaled[:, 0:HALF], wgs_rows[:, 0:HALF], ACT.Copy, scale=gain_rows[:, m : m + 1])
            weights.append(scaled)
        for s in range(2):
            nc.vector.tensor_copy(v1[s][:], words[1][:].indirect(pick[:, 32 * s : 32 * (s + 1)]))

        old_dealt = old[512:1024, :].rearrange("(p u e) t -> u p e t", u=2, e=2)
        for q in range(4):
            nc.sync.dma_start(
                w2_plane[32 * q : 32 * q + 4].bitcast(I32),
                w2_scales[:, 4 * q : 4 * q + 4, :].rearrange("a r c -> r a c").bitcast(I32),
            )
        old_low = [at(WORDS0 + 8 * KIB * e, "old_low%d" % e, [P, T2], F32) for e in range(2)]
        for e in range(2):
            nc.sync.dma_start(old_low[e][:], old_dealt[0][:, e, :])
        old_high = at(WORDS1, "old_high", [P, 2, T2], F32)
        nc.sync.dma_start(old_high[:], old_dealt[1])

        def first_stage_part(m, h, c0, width, b):
            acc = bank(b, "acc%d_%d" % (m, c0))
            cols = slice(c0, c0 + width)
            for a in range(2):
                codes, plane = stationary[m][a]
                moving = v0[:, cols] if a == 0 else v1[c0 // HALF][:, c0 % HALF : c0 % HALF + width]
                nc.tensor.matmul_mx(
                    out=acc[:, 0:width],
                    lhsT=codes.bitcast(FP8X4),
                    lhsT_scale=plane,
                    rhs=moving.bitcast(FP8X4),
                    rhs_scale=v_plane[:, a, cols],
                    start=(a == 0),
                    stop=(a == 1),
                )
            nc.scalar.activation(h, acc[:, 0:width], ACT.Tanh, scale=-1.0)

        def h_tile(slot, name):
            return at(H_RING + 4 * KIB * slot, name, [P, S], F32)

        def first_stage(m):
            if m in (3, 7):
                h = at(RAW_DEALT + (8 * KIB if m == 3 else 0), "h%d" % m, [P, S], F32)
            else:
                h = h_tile({1: 1, 2: 2, 4: 4, 5: 3, 6: 1}[m], "h%d" % m)
            for s in range(2):
                first_stage_part(m, h[:, HALF * s : HALF * (s + 1)], HALF * s, HALF, (0, 6, 0, 2, 6, 0, 2, 4)[m] + s)
            if m in (5, 6):
                nc.scalar.activation(h[:], h[:], ACT.Copy, scale=gain_dealt[:, m - 4 : m - 3])
            return h

        def weighted(m, h):
            product = h_tile((4, 3, 1)[m - 5], "product%d" % m)
            width = QUARTER if m == 7 else S
            for c0 in range(0, S, width):
                cols = slice(c0, c0 + width)
                nc.gpsimd.tensor_tensor(product[:, cols], h[:, cols], wgs_dealt[m - 4][:, cols], ALU.mult)
            return product

        def page_of(m):
            return pages[5 % PAGES] if m == 7 else pages[m % PAGES]

        def scatter(m, h):
            nc.vector.tensor_copy(page_of(m)[:].indirect(place[:]), h[:])

        def finish_weights(m):
            if m >= 2:
                weights.append(at(WEIGHTS + 4 * KIB * (m - 2), "weights%d" % m, [P, S], F32))
            cols = slice(HALF if m < 2 else 0, S)
            nc.scalar.activation(weights[m][:, cols], wgs_rows[:, cols], ACT.Copy, scale=gain_rows[:, m : m + 1])

        def scatter_weighted(m, h, factor, c0=0, width=S):
            nc.vector.tensor_tensor(
                page_of(m)[:].indirect(place[:, c0 // 16 : (c0 + width) // 16]), h, factor, ALU.mult
            )

        h_half = at(H_RING, "h0_first", [P, HALF], F32)
        for c0, b in ((0, 0), (QUARTER, 6)):
            cols = slice(c0, c0 + QUARTER)
            first_stage_part(0, h_half[:, cols], c0, QUARTER, b)
            scatter_weighted(0, h_half[:, cols], weights[0][:, cols], c0, QUARTER)
        quantize_natural(1)
        h_half = at(RAW_NATURAL + 6 * KIB, "h0_second", [P, HALF], F32)
        first_stage_part(0, h_half[:], HALF, HALF, 1)
        finish_weights(0)
        scatter_weighted(0, h_half[:], weights[0][:, HALF:S], HALF, HALF)

        turned = [at(RAW_NATURAL + 4 * KIB * ((c + 1) % CHUNKS), "turned%d" % c, [P, 4, 2, 256], BF16) for c in range(CHUNKS)]

        def difference_turned(m):
            for c in range(CHUNKS):
                acc = bank((2 + 4 * m + c) % 8, "fwd%d_%d" % (m, c))
                for step, source in enumerate((old_rows[m], pages[m % PAGES])):
                    for b in range(4):
                        t0 = BANK * c + P * b
                        nc.tensor.matmul(
                            acc[:, P * b : P * (b + 1)],
                            lhsT=source[:, t0 : t0 + P],
                            rhs=ident[:],
                            is_transpose=True,
                            start=(step == 0 and b == 0),
                            stop=(step == 1 and b == 3),
                        )
                nc.scalar.activation(
                    turned[c][:, :, :, 64 * m : 64 * (m + 1)].rearrange("p b u (w e) -> p u b w e", e=2),
                    acc[:].rearrange("p (b w u e) -> p u b w e", b=4, u=2, e=2),
                    ACT.Abs,
                )

        quantize_natural(2)
        h_next = first_stage(1)
        finish_weights(1)
        scatter_weighted(1, h_next[:], weights[1][:])
        quantize_natural(3)
        h_next = first_stage(2)
        difference_turned(0)
        finish_weights(2)
        scatter_weighted(2, h_next[:], weights[2][:])
        quantize_dealt()
        h_next = first_stage(3)
        difference_turned(1)
        finish_weights(3)
        scatter_weighted(3, h_next[:], weights[3][:])
        h_next = first_stage(4)
        h_after = first_stage(5)
        h_dealt = [h_tile(0, "product4")]
        difference_turned(2)
        nc.vector.scalar_tensor_tensor(
            h_dealt[0][:], h_next[:], gain_dealt[:, 0:1], wgs_dealt[0][:], ALU.mult, ALU.mult
        )
        h_dealt.append(weighted(5, h_after))
        scatter(4, h_dealt[0])
        h_dealt.extend([weighted(m, first_stage(m)) for m in (6, 7)])
        difference_turned(3)
        scatter(5, h_dealt[1])

        low = at(WGS_DEALT, "low", [P, 2, T2], F32)

        def sum_low(e):
            width = QUARTER if e == 0 else S
            for t0 in range(0, T2, width):
                cols = slice(t0, t0 + width)
                nc.gpsimd.tensor_tensor(low[:, e, cols], old_low[e][:, cols], pages[(4 + e) % PAGES][:, cols], ALU.add)

        sum_low(0)
        z_first = [at(RAW_DEALT + 8 * KIB * g, "z_first%d" % g, [P, 4096], BF16) for g in range(2)]
        for c in range(CHUNKS):
            for half in range(2):
                acc = bank((2 + 2 * c + half) % 8, "back%d_%d" % (c, half))
                for b in range(2):
                    for u in range(2):
                        col = P * (2 * b + u)
                        pairs = turned[c][:, 2 * half + b, u, :].bitcast(F32)
                        nc.tensor.transpose(acc[:, col : col + P], pairs, ident[:])
                z0 = 2048 * (c % 2) + 1024 * half
                nc.scalar.copy(
                    z_first[c // 2][:, z0 : z0 + 1024].bitcast(F32).rearrange("p (b t u) -> p b t u", b=2, u=2),
                    acc[:].rearrange("p (b u t) -> p b t u", b=2, u=2),
                )
        w2_codes = at(RAW_NATURAL, "w2_codes", [P, 2, 2 * N], U8)
        nc.sync.dma_start(w2_codes[:].bitcast(I32), w2_words.rearrange("a p c -> p a c").bitcast(I32))
        h_last = at(H_LAST, "h_last", [P, S], F32)
        nc.scalar.activation(h_last[:], h_dealt[3][:], ACT.Copy, scale=gain_dealt[:, 3:4])
        scatter(6, h_dealt[2])
        sum_low(1)
        first_codes = at(WEIGHTS, "first_codes", [P, T2], U32)
        first_plane = at(WEIGHTS + 8 * KIB, "first_plane", [P, T2], U8)
        for g in range(2):
            cols = slice(1024 * g, 1024 * (g + 1))
            nc.vector.quantize_mx(out=first_codes[:, cols].bitcast(FP8X4), scales=first_plane[:, cols], in_=z_first[g][:])
        scatter(7, h_last)

        def second_pass(acc, g, n, codes, plane, start, stop):
            nc.tensor.matmul_mx(
                out=acc,
                lhsT=w2_codes[:, g, 2 * P * n : 2 * P * (n + 1)].bitcast(FP4X4),
                lhsT_scale=w2_plane[:, g, P * n : P * (n + 1)],
                rhs=codes.bitcast(FP8X4),
                rhs_scale=plane,
                start=start,
                stop=stop,
            )

        pair_words, sums = [], []
        next_bank = 0
        sixth = []
        for k in range(0, len(PIECES), 2):
            t0, width = PIECES[k][0], PIECES[k][1] + PIECES[k + 1][1]
            cols = slice(t0, t0 + width)
            part = at(RAW_DEALT + 4 * t0, "sixth%d" % k, [P, width], F32)
            nc.gpsimd.tensor_tensor(part[:], old_high[:, 0, cols], pages[6 % PAGES][:, cols], ALU.add)
            sixth.extend([part[:, 0 : PIECES[k][1]], part[:, PIECES[k][1] : width]])
        for k, (t0, width) in enumerate(PIECES):
            cols = slice(t0, t0 + width)
            both = at(PAIR_WORDS + 8 * t0, "pair_words%d" % k, [P, 2, 2 * width], BF16)
            nc.scalar.activation(
                both[:, 0, :].rearrange("p (t e) -> p t e", e=2), low[:, :, cols].rearrange("p e t -> p t e"), ACT.Abs
            )
            pair_words.append(both)
            wide = width == BANK
            banks = [bank(next_bank + n, "sum%d_%d" % (k, n)) for n in range(2 if wide else 1)]
            next_bank = next_bank + len(banks)
            accs = [banks[n][:] if wide else banks[0][:, width * n : width * (n + 1)] for n in range(2)]
            for n in range(2):
                second_pass(accs[n], 0, n, first_codes[:, cols], first_plane[:, cols], wide or n == 0, False)
            sums.append((banks, accs))
        for k, (t0, width) in enumerate(PIECES):
            nc.scalar.activation(pair_words[k][:, 1, 0 : 2 * width : 2], sixth[k], ACT.Abs)

        out_rows = out.rearrange("(n p) t -> p n t", p=P)
        seventh, woven, staged = {}, {}, {}

        def add_last(k):
            t0, width = PIECES[k]
            cols = slice(t0, t0 + width)
            seventh[k] = at(RAW_DEALT + 4 * t0, "seventh%d" % k, [P, width], F32)
            nc.vector.tensor_tensor(seventh[k][:], old_high[:, 1, cols], page_of(7)[:, cols], ALU.add)

        def abs_last(k):
            nc.scalar.activation(pair_words[k][:, 1, 1 : 2 * PIECES[k][1] : 2], seventh[k][:], ACT.Abs)

        def weave(k):
            t0, width = PIECES[k]
            woven[k] = at(OLD_ROWS + 8 * t0, "z_second%d" % k, [P, 4 * width], BF16)
            nc.vector.tensor_copy(
                woven[k][:].bitcast(I32).rearrange("p (t u) -> p t u", u=2),
                pair_words[k][:].bitcast(I32).rearrange("p u t -> p t u"),
            )

        def finish(k):
            width = PIECES[k][1]
            wide = width == BANK
            codes = sb("second_codes%d" % k, [P, width], U32)
            plane = sb("second_plane%d" % k, [P, width], U8)
            nc.vector.quantize_mx(out=codes[:].bitcast(FP8X4), scales=plane[:], in_=woven[k][:])
            for n in range(2):
                second_pass(sums[k][1][n], 1, n, codes[:], plane[:], False, wide or n == 1)

        def store(k, n, copy):
            t0, width = PIECES[k]
            cols = slice(t0, t0 + width)
            banks, accs = sums[k]
            if k not in staged:
                staged[k] = at(WORDS0 + 8 * t0, "staged%d" % k, [P, 2, width], F32)
            if width == BANK:
                copy(staged[k][:, n, :], accs[n])
                nc.sync.dma_start(out_rows[:, n, cols], staged[k][:, n, :])
            else:
                copy(staged[k][:].rearrange("p n t -> p (n t)"), banks[0][:])
                nc.sync.dma_start(out_rows[:, :, cols], staged[k][:])

        add_last(0)
        add_last(1)
        add_last(2)
        abs_last(0)
        abs_last(1)
        abs_last(2)
        weave(0)
        add_last(3)
        add_last(4)
        abs_last(3)
        abs_last(4)
        finish(0)
        weave(1)
        add_last(5)
        store(0, 0, nc.scalar.copy)
        abs_last(5)
        finish(1)
        weave(2)
        weave(3)
        store(1, 0, nc.scalar.copy)
        store(1, 1, nc.scalar.copy)
        finish(2)
        finish(3)
        weave(4)
        weave(5)
        finish(4)
        finish(5)
        store(2, 0, nc.scalar.copy)
        store(2, 1, nc.scalar.copy)
        store(3, 0, nc.vector.tensor_copy)
        store(4, 0, nc.scalar.copy)
        store(5, 0, nc.vector.tensor_copy)
